import numpy as np
import ml_dtypes


def mxq(x, axis, fmt="e4m3"):
    dtype, down = {"e4m3": (ml_dtypes.float8_e4m3fn, 7), "e5m2": (ml_dtypes.float8_e5m2, 14)}[fmt]
    v = np.moveaxis(np.asarray(x, np.float32).astype(ml_dtypes.bfloat16).astype(np.float64), axis, -1)
    blocks = v.reshape(v.shape[:-1] + (-1, 32))
    amax = np.abs(blocks).max(-1, keepdims=True)
    byte = np.maximum(np.where(amax > 0, np.frexp(amax)[1] - 1 + 127, 0) - down, 1)
    scale = np.exp2(byte - 127.0)
    codes = (blocks / scale).astype(np.float32).astype(dtype).astype(np.float64)
    return np.moveaxis((codes * scale).reshape(v.shape), -1, axis)


WIDE = False


def mx_kscale(k):
    if not WIDE:
        return np.ones(k)
    levels = np.array([10, -10, 5, -5, 0])
    if k % 512:
        return np.exp2(np.random.permutation(np.resize(levels, k // 32))).repeat(32)
    a = np.empty((k // 512, 16))
    for p in range(k // 512):
        a[p, :8] = np.random.permutation(np.resize(levels, 8))
        for g in range(8):
            far = levels[np.abs(levels - a[p, g]) >= 10]
            a[p, g + 8] = far[np.random.randint(len(far))]
    return np.exp2(a.ravel()).repeat(32)


def f64(x):
    return np.asarray(x).astype(np.float64)


def striped(idx):
    return np.tile(idx.reshape(-1, 16).T, (8, 1)).astype(np.uint16)


def unstriped(offs):
    return offs[:16].T.reshape(-1).astype(np.int64)


def pack_weight(w):
    k, n = w.shape
    w = f64(np.asarray(w, np.float32).astype(ml_dtypes.bfloat16)).reshape(k // 32, 32, n)
    amax = np.abs(w).max(1)
    byte = np.clip(np.where(amax > 0, np.frexp(amax)[1] - 1 + 127 - 7, 1), 1, 254)
    scaled = (w * np.exp2(127.0 - byte)[:, None, :]).reshape(k, n).astype(np.float32)
    words = np.ascontiguousarray(scaled.reshape(k // 512, 128, 4, n).transpose(0, 1, 3, 2)).astype(ml_dtypes.float8_e4m3fn).view(np.uint8)
    return words, np.ascontiguousarray(byte.astype(np.uint8).reshape(k // 512, 16, n))


def unpack_weight(words, scales):
    g, p, n, _ = words.shape
    vals = np.ascontiguousarray(words).view(ml_dtypes.float8_e4m3fn).astype(np.float64) * np.repeat(np.exp2(scales.astype(np.float64) - 127.0), 8, axis=1)[..., None]
    return vals.transpose(0, 1, 3, 2).reshape(g * 512, n)


E2M1 = np.array([0.0, 0.5, 1.0, 1.5, 2.0, 3.0, 4.0, 6.0, -0.0, -0.5, -1.0, -1.5, -2.0, -3.0, -4.0, -6.0])


def pack_fp4(w):
    k, n = w.shape
    w = f64(np.asarray(w, np.float32).astype(ml_dtypes.bfloat16)).reshape(k // 32, 32, n)
    amax = np.abs(w).max(1)
    mant, ex = np.frexp(amax / 6.0)
    byte = np.clip(np.where(amax > 0, np.where(mant > 0.5, ex, ex - 1) + 127, 1), 1, 254)
    scaled = (w * np.exp2(127.0 - byte)[:, None, :]).reshape(k, n).astype(np.float32)
    c = np.ascontiguousarray(scaled.reshape(k // 512, 128, 4, n).transpose(0, 1, 3, 2)).astype(ml_dtypes.float4_e2m1fn).view(np.uint8) & 0xF
    words = (c[..., 0::2] | (c[..., 1::2] << 4)).reshape(k // 512, 128, 2 * n)
    return np.ascontiguousarray(words), np.ascontiguousarray(byte.astype(np.uint8).reshape(k // 512, 16, n))


def unpack_fp4(words, scales):
    g, _, n = scales.shape
    words = np.ascontiguousarray(words).reshape(g, 128, n, 2)
    nib = np.empty((g, 128, n, 4), np.uint8)
    nib[..., 0::2] = words & 0xF
    nib[..., 1::2] = words >> 4
    vals = E2M1[nib] * np.repeat(np.exp2(scales.astype(np.float64) - 127.0), 8, axis=1)[..., None]
    return vals.transpose(0, 1, 3, 2).reshape(g * 512, n)


def planes(y):
    n, m = y.shape
    v = y.astype(np.float32).astype(ml_dtypes.bfloat16).astype(np.float64).reshape(n // 32, 32, m)
    top = np.abs(v).max(1)
    byte = np.clip(np.where(top > 0, np.frexp(top)[1] - 1 + 127 - 7, 1), 1, 254)
    codes = (v * np.exp2(127.0 - byte)[:, None, :]).reshape(n, m).astype(np.float32).astype(ml_dtypes.float8_e4m3fn).view(np.uint8)
    words = codes.reshape(n // 512, 128, 4, m).transpose(0, 1, 3, 2)
    return np.ascontiguousarray(words), np.ascontiguousarray(byte.astype(np.uint8).reshape(n // 512, 16, m))


def gelu(v):
    return 0.5 * v * (1.0 + np.tanh(np.sqrt(2.0 / np.pi) * (v + 0.044715 * v**3)))


K, T, S, H = 1024, 2048, 1024, 512


def setup_inputs():
    n = np.random.standard_normal
    s = mx_kscale(K)[:, None]
    u = mx_kscale(H)
    packed_xT = pack_weight(n((K, T)) * s)
    packed_w2 = pack_fp4(n((H, H)) / np.sqrt(H) / u[:, None])
    return {
        "x_words": packed_xT[0],
        "x_scales": packed_xT[1],
        "w1": (n((K, H)) / np.sqrt(K) / s * u).astype(np.float32),
        "w2_words": packed_w2[0],
        "w2_scales": packed_w2[1],
        "turn": (np.random.uniform(0.5, 1.5, (H, 1)) * u[:, None]).astype(np.float32),
        "offs": striped(np.random.permutation(T)[:S]),
    }


def reference(x_words, x_scales, w1, w2_words, w2_scales, turn, offs):
    xq = unpack_weight(x_words, x_scales)[:, unstriped(offs)]
    h = mxq(f64(w1), 0, "e4m3").T @ xq
    g = gelu(h)
    y = unpack_fp4(w2_words, w2_scales).T @ mxq(g, 0, "e4m3")
    out_0 = h + f64(turn) * y
    return (out_0,) + planes(out_0)

@@ -1,0 +1,226 @@
+from contextlib import ExitStack
+
+import concourse.mybir as mybir
+
+K, T, S, H = 1024, 2048, 1024, 512
+FLOPS = 2 * K * H * S + 2 * H * H * S
+
+F32 = mybir.dt.float32
+BF16 = mybir.dt.bfloat16
+I32 = mybir.dt.int32
+U32 = mybir.dt.uint32
+U16 = mybir.dt.uint16
+U8 = mybir.dt.uint8
+FP8X4 = mybir.dt.float8_e4m3fn_x4
+FP4X4 = mybir.dt.float4_e2m1fn_x4
+GELU = mybir.ActivationFunctionType.Gelu_apprx_tanh
+MULT = mybir.AluOpType.mult
+ADD = mybir.AluOpType.add
+
+P = 128
+PACK = 4
+PASSES = K // (P * PACK)
+QUADS = 4
+BLOCK = 128
+GATHER = 256
+CHUNKS = (128, 128, 256, 256, 128, 128)
+H_ON_VECTOR = ()
+CAST_ON_SCALAR = (4, 5)
+H_BANKS = 3
+Y_BANKS = 4
+WARM_PASSES = 6
+SCALAR_SHARE = 96
+
+
+def tile_picked_zres_gelu_po_kernel(
+    tc, x_words, x_scales, w1, w2_words, w2_scales, turn, offs, out_0, out_1, out_2
+):
+    nc = tc.nc
+    with ExitStack() as ctx:
+        keep = ctx.enter_context(tc.tile_pool(name="keep", bufs=1))
+        psum = ctx.enter_context(tc.psum_pool(name="psum", bufs=4))
+
+        offsets = keep.tile([P, S // 16], U16, name="offsets")
+        x_plane = keep.tile([P, T], U8, name="x_plane", align_bytes=64)
+        w2_plane_raw = keep.tile([P, H], U8, name="w2_plane_raw", align_bytes=64)
+        warm = keep.tile([P, 8], F32, name="warm")
+        warm_out = keep.tile([P, 8], F32, name="warm_out")
+        nc.vector.memset(x_plane[:].bitcast(I32), 0)
+        nc.vector.memset(w2_plane_raw[:].bitcast(I32), 0)
+        nc.vector.memset(warm[:], 0.0)
+        nc.scalar.activation(warm_out[:], warm[:], GELU)
+
+        w1_raw = [keep.tile([P, PACK, H], F32, name="w1_raw%d" % a) for a in range(PASSES)]
+        x_table = [keep.tile([P, T], U32, name="x_table%d" % a, align_bytes=64) for a in range(PASSES)]
+        w2_raw = keep.tile([P, 2 * H], U8, name="w2_raw", align_bytes=64)
+        factor = keep.tile([P, PACK], F32, name="factor")
+
+        def load_w1(a):
+            nc.sync.dma_start(w1_raw[a][:], w1[a * 512 : (a + 1) * 512, :].rearrange("(p j) c -> p j c", j=PACK))
+
+        def load_x(a):
+            nc.sync.dma_start(x_table[a][:].bitcast(I32), x_words[a].rearrange("p n t -> p (n t)").bitcast(I32))
+
+        nc.sync.dma_start(offsets[:], offs)
+        nc.sync.dma_start(w2_raw[:].bitcast(I32), w2_words[0].bitcast(I32))
+        for q in range(QUADS):
+            nc.sync.dma_start(
+                x_plane[32 * q : 32 * q + 8, :].bitcast(I32), x_scales[:, 4 * q : 4 * q + 4, :].bitcast(I32)
+            )
+        load_w1(0)
+        load_x(0)
+        load_w1(1)
+        for q in range(QUADS):
+            nc.sync.dma_start(
+                w2_plane_raw[32 * q : 32 * q + 4, :].bitcast(I32), w2_scales[0, 4 * q : 4 * q + 4, :].bitcast(I32)
+            )
+        load_x(1)
+        nc.sync.dma_start(factor[:], turn.rearrange("(p t) o -> p (t o)", t=PACK))
+
+        w1_bf = [
+            keep.tile([P, H * PACK], BF16, name="w1_bf%d" % a, tag="staged%d" % a, align_bytes=64) for a in range(PASSES)
+        ]
+        w1_codes = [keep.tile([P, H], U32, name="w1_codes%d" % a, align_bytes=64) for a in range(PASSES)]
+        w1_plane = [keep.tile([P, H], U8, name="w1_plane%d" % a, align_bytes=64) for a in range(PASSES)]
+        x_picked = {}
+        x_picked_plane = keep.tile([P, S], U8, name="x_picked_plane", align_bytes=64)
+        w2_codes = keep.tile([P, 2 * H], U8, name="w2_codes", align_bytes=64)
+        w2_plane = keep.tile([P, H], U8, name="w2_plane", align_bytes=64)
+
+        def w1_views(a, m0, m1):
+            dst = w1_bf[a][:].rearrange("p (t m j) -> p m j t", t=PACK, j=PACK)[:, m0:m1]
+            src = w1_raw[a][:].rearrange("p j (m t) -> p m j t", t=PACK)[:, m0:m1]
+            return dst, src
+
+        def quantize_w1(a):
+            nc.vector.quantize_mx(w1_codes[a][:].bitcast(FP8X4), w1_plane[a][:], w1_bf[a][:])
+
+        def gather_x(a, n0, n1, tag):
+            picked = keep.tile([P, n1 - n0], U32, name="x_picked", tag=tag, align_bytes=64)
+            nc.vector.tensor_copy(picked[:], x_table[a][:].indirect(offsets[:, n0 // 16 : n1 // 16]))
+            for n in range(n0, n1, BLOCK):
+                x_picked[a, n] = picked[:, n - n0 : n - n0 + BLOCK]
+            return picked
+
+        nc.scalar.copy(*w1_views(0, 0, P))
+        nc.vector.tensor_copy(
+            w2_codes[:].rearrange("p (t m b) -> p t m b", t=PACK, b=2),
+            w2_raw[:].rearrange("p (m t b) -> p t m b", t=PACK, b=2),
+        )
+        nc.vector.tensor_copy(x_picked_plane[:], x_plane[:].indirect(offsets[:]))
+        first_picked = gather_x(0, 0, S // 2, "picked0")
+        quantize_w1(0)
+        gather_x(0, S // 2, S, "staged0")
+        idle_bank = psum.tile([P, 512], F32, name="idle_bank", bufs=1)
+        for turn_number in range(WARM_PASSES):
+            nc.tensor.matmul_mx(
+                idle_bank[:],
+                lhsT=w1_codes[0][:, 0:P].bitcast(FP8X4),
+                lhsT_scale=w1_plane[0][:, 0:P],
+                rhs=first_picked[:].bitcast(FP8X4),
+                rhs_scale=x_picked_plane[:, 0:512],
+                start=True,
+                stop=True,
+            )
+        nc.scalar.copy(*w1_views(1, 0, SCALAR_SHARE))
+        nc.vector.tensor_copy(*w1_views(1, SCALAR_SHARE, P))
+        nc.vector.tensor_copy(
+            w2_plane[:].rearrange("p (t m) -> p t m", t=PACK),
+            w2_plane_raw[:].rearrange("p (m t) -> p t m", t=PACK),
+        )
+        quantize_w1(1)
+
+        out_codes = keep.tile([P, S], U32, name="out_codes", align_bytes=64)
+        out_plane = keep.tile([P, S], U8, name="out_plane", align_bytes=64)
+        out_rows = out_0.rearrange("(p t) n -> p t n", t=PACK)
+        out_words = out_1[0].rearrange("p n t -> p (n t)").bitcast(I32)
+
+        starts = [sum(CHUNKS[:c]) for c in range(len(CHUNKS))]
+        h_kept = [keep.tile([P, PACK, w], F32, name="h_kept%d" % c) for c, w in enumerate(CHUNKS)]
+        g_bf = [keep.tile([P, w * PACK], BF16, name="g_bf%d" % c, align_bytes=64) for c, w in enumerate(CHUNKS)]
+        g_codes = [keep.tile([P, w], U32, name="g_codes%d" % c, align_bytes=64) for c, w in enumerate(CHUNKS)]
+        g_plane = [keep.tile([P, w], U8, name="g_plane%d" % c, align_bytes=64) for c, w in enumerate(CHUNKS)]
+        result = [keep.tile([P, PACK, w], F32, name="result%d" % c) for c, w in enumerate(CHUNKS)]
+        result_bf = [keep.tile([P, w * PACK], BF16, name="result_bf%d" % c, align_bytes=64) for c, w in enumerate(CHUNKS)]
+
+        def project(c):
+            banks = []
+            for n0 in range(starts[c], starts[c] + CHUNKS[c], BLOCK):
+                if n0 % GATHER == 0:
+                    gather_x(1, n0, n0 + GATHER, "staged1" if n0 == 0 else "picked1_%d" % n0)
+                bank = psum.tile([P, PACK, BLOCK], F32, name="h_bank", bufs=H_BANKS)
+                for t in range(PACK):
+                    for a in range(PASSES):
+                        nc.tensor.matmul_mx(
+                            bank[:, t, :],
+                            lhsT=w1_codes[a][:, t * P : (t + 1) * P].bitcast(FP8X4),
+                            lhsT_scale=w1_plane[a][:, t * P : (t + 1) * P],
+                            rhs=x_picked[a, n0].bitcast(FP8X4),
+                            rhs_scale=x_picked_plane[4 * a : P, n0 : n0 + BLOCK],
+                            start=(a == 0),
+                            stop=(a == PASSES - 1),
+                        )
+                local = n0 - starts[c]
+                nc.scalar.activation(
+                    g_bf[c][:, local * PACK : (local + BLOCK) * PACK].rearrange("p (n t) -> p n t", t=PACK),
+                    bank[:].rearrange("p t n -> p n t"),
+                    GELU,
+                )
+                banks.append((n0, local, bank))
+            for n0, local, bank in banks:
+                if n0 // BLOCK in H_ON_VECTOR:
+                    nc.vector.tensor_copy(h_kept[c][:, :, local : local + BLOCK], bank[:])
+                else:
+                    nc.scalar.copy(h_kept[c][:, :, local : local + BLOCK], bank[:])
+
+        def quantize_g(c):
+            nc.vector.quantize_mx(g_codes[c][:].bitcast(FP8X4), g_plane[c][:], g_bf[c][:])
+
+        def branch(c):
+            w = CHUNKS[c]
+            per_bank = 512 // w
+            for t0 in range(0, PACK, per_bank):
+                bank = psum.tile([P, 512], F32, name="y_bank", bufs=Y_BANKS)
+                for t in range(t0, t0 + per_bank):
+                    nc.tensor.matmul_mx(
+                        bank[:, (t - t0) * w : (t - t0 + 1) * w],
+                        lhsT=w2_codes[:, t * 2 * P : (t + 1) * 2 * P].bitcast(FP4X4),
+                        lhsT_scale=w2_plane[:, t * P : (t + 1) * P],
+                        rhs=g_codes[c][:].bitcast(FP8X4),
+                        rhs_scale=g_plane[c][:],
+                        start=True,
+                        stop=True,
+                    )
+                for t in range(t0, t0 + per_bank):
+                    nc.vector.scalar_tensor_tensor(
+                        result[c][:, t, :],
+                        bank[:, (t - t0) * w : (t - t0 + 1) * w],
+                        factor[:, t : t + 1],
+                        h_kept[c][:, t, :],
+                        MULT,
+                        ADD,
+                    )
+            nc.sync.dma_start(out_rows[:, :, starts[c] : starts[c] + w], result[c][:])
+
+        def round_result(c):
+            dst = result_bf[c][:].rearrange("p (n i t) -> p n t i", i=4, t=PACK)
+            src = result[c][:].rearrange("p t (n i) -> p n t i", i=4)
+            if c in CAST_ON_SCALAR:
+                nc.scalar.copy(dst, src)
+            else:
+                nc.vector.tensor_copy(dst, src)
+
+        def quantize_result(c):
+            cols = slice(starts[c], starts[c] + CHUNKS[c])
+            nc.vector.quantize_mx(out_codes[:, cols].bitcast(FP8X4), out_plane[:, cols], result_bf[c][:])
+            nc.sync.dma_start(out_words[:, cols], out_codes[:, cols].bitcast(I32))
+
+        stages = (project, quantize_g, branch, round_result, quantize_result)
+        for step in range(len(CHUNKS) + len(stages) - 1):
+            for s, stage in reversed(list(enumerate(stages))):
+                if 0 <= step - s < len(CHUNKS):
+                    stage(step - s)
+
+        for q in range(QUADS):
+            queue = nc.sync if q % 2 == 0 else nc.scalar
+            queue.dma_start(out_2[0, 4 * q : 4 * q + 4, :].bitcast(I32), out_plane[32 * q : 32 * q + 4, :].bitcast(I32))

@@ -23,13 +23,14 @@ PASSES = K // (P * PACK)
 QUADS = 4
 BLOCK = 128
 GATHER = 256
-CHUNKS = (128, 128, 256, 256, 128, 128)
-H_ON_VECTOR = ()
-CAST_ON_SCALAR = (4, 5)
-H_BANKS = 3
+CHUNKS = (256, 256, 256, 128, 128)
+H_ON_VECTOR = (0,)
+CAST_ON_SCALAR = (2, 3)
+H_BANKS = 4
 Y_BANKS = 4
-WARM_PASSES = 6
-SCALAR_SHARE = 96
+WARM_PASSES = 4
+CODE_STORES = {1: 0, 3: 2, 4: 4}
+SCALAR_SHARE = (96, 80)
 
 
 def tile_picked_zres_gelu_po_kernel(
@@ -58,23 +59,25 @@ def tile_picked_zres_gelu_po_kernel(
         def load_w1(a):
             nc.sync.dma_start(w1_raw[a][:], w1[a * 512 : (a + 1) * 512, :].rearrange("(p j) c -> p j c", j=PACK))
 
-        def load_x(a):
-            nc.sync.dma_start(x_table[a][:].bitcast(I32), x_words[a].rearrange("p n t -> p (n t)").bitcast(I32))
+        def load_x(a, n0, n1):
+            words = x_words[a].rearrange("p n t -> p (n t)").bitcast(I32)
+            nc.sync.dma_start(x_table[a][:, n0:n1].bitcast(I32), words[:, n0:n1])
 
         nc.sync.dma_start(offsets[:], offs)
         nc.sync.dma_start(w2_raw[:].bitcast(I32), w2_words[0].bitcast(I32))
+        load_x(0, 0, T // 2)
         for q in range(QUADS):
             nc.sync.dma_start(
                 x_plane[32 * q : 32 * q + 8, :].bitcast(I32), x_scales[:, 4 * q : 4 * q + 4, :].bitcast(I32)
             )
+        load_x(0, T // 2, T)
         load_w1(0)
-        load_x(0)
         load_w1(1)
         for q in range(QUADS):
             nc.sync.dma_start(
                 w2_plane_raw[32 * q : 32 * q + 4, :].bitcast(I32), w2_scales[0, 4 * q : 4 * q + 4, :].bitcast(I32)
             )
-        load_x(1)
+        load_x(1, 0, T)
         nc.sync.dma_start(factor[:], turn.rearrange("(p t) o -> p (t o)", t=PACK))
 
         w1_bf = [
@@ -95,40 +98,41 @@ def tile_picked_zres_gelu_po_kernel(
         def quantize_w1(a):
             nc.vector.quantize_mx(w1_codes[a][:].bitcast(FP8X4), w1_plane[a][:], w1_bf[a][:])
 
-        def gather_x(a, n0, n1, tag):
-            picked = keep.tile([P, n1 - n0], U32, name="x_picked", tag=tag, align_bytes=64)
-            nc.vector.tensor_copy(picked[:], x_table[a][:].indirect(offsets[:, n0 // 16 : n1 // 16]))
+        def gather_x(a, n0, picked):
+            n1 = n0 + picked.shape[1]
+            nc.vector.tensor_copy(picked, x_table[a][:].indirect(offsets[:, n0 // 16 : n1 // 16]))
             for n in range(n0, n1, BLOCK):
                 x_picked[a, n] = picked[:, n - n0 : n - n0 + BLOCK]
-            return picked
 
-        nc.scalar.copy(*w1_views(0, 0, P))
         nc.vector.tensor_copy(
             w2_codes[:].rearrange("p (t m b) -> p t m b", t=PACK, b=2),
             w2_raw[:].rearrange("p (m t b) -> p t m b", t=PACK, b=2),
         )
         nc.vector.tensor_copy(x_picked_plane[:], x_plane[:].indirect(offsets[:]))
-        first_picked = gather_x(0, 0, S // 2, "picked0")
+        first_picked = keep.tile([P, S], U32, name="first_picked", align_bytes=64)
+        gather_x(0, 0, first_picked[:])
+        nc.scalar.copy(*w1_views(0, 0, SCALAR_SHARE[0]))
+        nc.vector.tensor_copy(*w1_views(0, SCALAR_SHARE[0], P))
         quantize_w1(0)
-        gather_x(0, S // 2, S, "staged0")
-        idle_bank = psum.tile([P, 512], F32, name="idle_bank", bufs=1)
+        idle_bank = psum.tile([P, 512], F32, name="y_bank", bufs=Y_BANKS)
         for turn_number in range(WARM_PASSES):
             nc.tensor.matmul_mx(
                 idle_bank[:],
                 lhsT=w1_codes[0][:, 0:P].bitcast(FP8X4),
                 lhsT_scale=w1_plane[0][:, 0:P],
-                rhs=first_picked[:].bitcast(FP8X4),
+                rhs=first_picked[:, 0:512].bitcast(FP8X4),
                 rhs_scale=x_picked_plane[:, 0:512],
                 start=True,
                 stop=True,
             )
-        nc.scalar.copy(*w1_views(1, 0, SCALAR_SHARE))
-        nc.vector.tensor_copy(*w1_views(1, SCALAR_SHARE, P))
+        nc.scalar.copy(*w1_views(1, 0, SCALAR_SHARE[1]))
+        nc.vector.tensor_copy(*w1_views(1, SCALAR_SHARE[1], P))
         nc.vector.tensor_copy(
             w2_plane[:].rearrange("p (t m) -> p t m", t=PACK),
             w2_plane_raw[:].rearrange("p (m t) -> p t m", t=PACK),
         )
         quantize_w1(1)
+        last_picked = keep.tile([P, S - GATHER], U32, name="last_picked", tag="staged1", align_bytes=64)
 
         out_codes = keep.tile([P, S], U32, name="out_codes", align_bytes=64)
         out_plane = keep.tile([P, S], U8, name="out_plane", align_bytes=64)
@@ -137,7 +141,9 @@ def tile_picked_zres_gelu_po_kernel(
 
         starts = [sum(CHUNKS[:c]) for c in range(len(CHUNKS))]
         h_kept = [keep.tile([P, PACK, w], F32, name="h_kept%d" % c) for c, w in enumerate(CHUNKS)]
-        g_bf = [keep.tile([P, w * PACK], BF16, name="g_bf%d" % c, align_bytes=64) for c, w in enumerate(CHUNKS)]
+        g_bf = [
+            keep.tile([P, w * PACK], BF16, name="g_bf", tag="g_bf%d" % c, align_bytes=64) for c, w in enumerate(CHUNKS)
+        ]
         g_codes = [keep.tile([P, w], U32, name="g_codes%d" % c, align_bytes=64) for c, w in enumerate(CHUNKS)]
         g_plane = [keep.tile([P, w], U8, name="g_plane%d" % c, align_bytes=64) for c, w in enumerate(CHUNKS)]
         result = [keep.tile([P, PACK, w], F32, name="result%d" % c) for c, w in enumerate(CHUNKS)]
@@ -146,8 +152,11 @@ def tile_picked_zres_gelu_po_kernel(
         def project(c):
             banks = []
             for n0 in range(starts[c], starts[c] + CHUNKS[c], BLOCK):
-                if n0 % GATHER == 0:
-                    gather_x(1, n0, n0 + GATHER, "staged1" if n0 == 0 else "picked1_%d" % n0)
+                if n0 == S - GATHER:
+                    tail_picked = keep.tile([P, GATHER], U32, name="tail_picked", tag="g_bf0", align_bytes=64)
+                    gather_x(1, n0, tail_picked[:])
+                elif n0 % GATHER == 0:
+                    gather_x(1, n0, last_picked[:, n0 : n0 + GATHER])
                 bank = psum.tile([P, PACK, BLOCK], F32, name="h_bank", bufs=H_BANKS)
                 for t in range(PACK):
                     for a in range(PASSES):
@@ -205,7 +214,11 @@ def tile_picked_zres_gelu_po_kernel(
         def round_result(c):
             dst = result_bf[c][:].rearrange("p (n i t) -> p n t i", i=4, t=PACK)
             src = result[c][:].rearrange("p t (n i) -> p n t i", i=4)
-            if c in CAST_ON_SCALAR:
+            if c == len(CHUNKS) - 1:
+                half = CHUNKS[c] // 8
+                nc.scalar.copy(dst[:, :half], src[:, :half])
+                nc.vector.tensor_copy(dst[:, half:], src[:, half:])
+            elif c in CAST_ON_SCALAR:
                 nc.scalar.copy(dst, src)
             else:
                 nc.vector.tensor_copy(dst, src)
@@ -213,7 +226,9 @@ def tile_picked_zres_gelu_po_kernel(
         def quantize_result(c):
             cols = slice(starts[c], starts[c] + CHUNKS[c])
             nc.vector.quantize_mx(out_codes[:, cols].bitcast(FP8X4), out_plane[:, cols], result_bf[c][:])
-            nc.sync.dma_start(out_words[:, cols], out_codes[:, cols].bitcast(I32))
+            if c in CODE_STORES:
+                cols = slice(starts[CODE_STORES[c]], cols.stop)
+                nc.sync.dma_start(out_words[:, cols], out_codes[:, cols].bitcast(I32))
 
         stages = (project, quantize_g, branch, round_result, quantize_result)
         for step in range(len(CHUNKS) + len(stages) - 1):

@@ -30,7 +30,7 @@ H_BANKS = 4
 Y_BANKS = 4
 WARM_PASSES = 4
 CODE_STORES = {1: 0, 3: 2, 4: 4}
-SCALAR_SHARE = (96, 80)
+SCALAR_SHARE = (128, 64)
 
 
 def tile_picked_zres_gelu_po_kernel(
@@ -39,10 +39,11 @@ def tile_picked_zres_gelu_po_kernel(
     nc = tc.nc
     with ExitStack() as ctx:
         keep = ctx.enter_context(tc.tile_pool(name="keep", bufs=1))
+        shared = ctx.enter_context(tc.tile_pool(name="shared", bufs=1))
         psum = ctx.enter_context(tc.psum_pool(name="psum", bufs=4))
 
         offsets = keep.tile([P, S // 16], U16, name="offsets")
-        x_plane = keep.tile([P, T], U8, name="x_plane", align_bytes=64)
+        x_plane = shared.tile([P, T], U8, name="x_plane", align_bytes=64, offset=1024)
         w2_plane_raw = keep.tile([P, H], U8, name="w2_plane_raw", align_bytes=64)
         warm = keep.tile([P, 8], F32, name="warm")
         warm_out = keep.tile([P, 8], F32, name="warm_out")
@@ -56,8 +57,9 @@ def tile_picked_zres_gelu_po_kernel(
         w2_raw = keep.tile([P, 2 * H], U8, name="w2_raw", align_bytes=64)
         factor = keep.tile([P, PACK], F32, name="factor")
 
-        def load_w1(a):
-            nc.sync.dma_start(w1_raw[a][:], w1[a * 512 : (a + 1) * 512, :].rearrange("(p j) c -> p j c", j=PACK))
+        def load_w1(a, j0, j1):
+            rows = w1[a * 512 : (a + 1) * 512, :].rearrange("(p j) c -> p j c", j=PACK)
+            nc.sync.dma_start(w1_raw[a][:, j0:j1, :], rows[:, j0:j1, :])
 
         def load_x(a, n0, n1):
             words = x_words[a].rearrange("p n t -> p (n t)").bitcast(I32)
@@ -65,14 +67,21 @@ def tile_picked_zres_gelu_po_kernel(
 
         nc.sync.dma_start(offsets[:], offs)
         nc.sync.dma_start(w2_raw[:].bitcast(I32), w2_words[0].bitcast(I32))
+        def load_x_scales(r):
+            for a in range(PASSES):
+                nc.sync.dma_start(
+                    x_plane[4 * a + r : P : 32, :].bitcast(I32), x_scales[a, r : 16 : 4, :].bitcast(I32)
+                )
+
         load_x(0, 0, T // 2)
-        for q in range(QUADS):
-            nc.sync.dma_start(
-                x_plane[32 * q : 32 * q + 8, :].bitcast(I32), x_scales[:, 4 * q : 4 * q + 4, :].bitcast(I32)
-            )
+        load_x_scales(0)
+        load_x_scales(1)
         load_x(0, T // 2, T)
-        load_w1(0)
-        load_w1(1)
+        load_w1(0, 0, 2)
+        load_x_scales(2)
+        load_x_scales(3)
+        load_w1(0, 2, PACK)
+        load_w1(1, 0, PACK)
         for q in range(QUADS):
             nc.sync.dma_start(
                 w2_plane_raw[32 * q : 32 * q + 4, :].bitcast(I32), w2_scales[0, 4 * q : 4 * q + 4, :].bitcast(I32)
@@ -81,9 +90,13 @@ def tile_picked_zres_gelu_po_kernel(
         nc.sync.dma_start(factor[:], turn.rearrange("(p t) o -> p (t o)", t=PACK))
 
         w1_bf = [
-            keep.tile([P, H * PACK], BF16, name="w1_bf%d" % a, tag="staged%d" % a, align_bytes=64) for a in range(PASSES)
+            keep.tile([P, H * PACK], BF16, name="w1_bf0", align_bytes=64),
+            shared.tile([P, H * PACK], BF16, name="w1_bf1", align_bytes=64, offset=2048),
         ]
-        w1_codes = [keep.tile([P, H], U32, name="w1_codes%d" % a, align_bytes=64) for a in range(PASSES)]
+        w1_codes = [
+            shared.tile([P, H], U32, name="w1_codes0", align_bytes=64, offset=0),
+            keep.tile([P, H], U32, name="w1_codes1", align_bytes=64),
+        ]
         w1_plane = [keep.tile([P, H], U8, name="w1_plane%d" % a, align_bytes=64) for a in range(PASSES)]
         x_picked = {}
         x_picked_plane = keep.tile([P, S], U8, name="x_picked_plane", align_bytes=64)
@@ -108,11 +121,10 @@ def tile_picked_zres_gelu_po_kernel(
             w2_codes[:].rearrange("p (t m b) -> p t m b", t=PACK, b=2),
             w2_raw[:].rearrange("p (m t b) -> p t m b", t=PACK, b=2),
         )
-        nc.vector.tensor_copy(x_picked_plane[:], x_plane[:].indirect(offsets[:]))
         first_picked = keep.tile([P, S], U32, name="first_picked", align_bytes=64)
         gather_x(0, 0, first_picked[:])
+        nc.vector.tensor_copy(x_picked_plane[:], x_plane[:].indirect(offsets[:]))
         nc.scalar.copy(*w1_views(0, 0, SCALAR_SHARE[0]))
-        nc.vector.tensor_copy(*w1_views(0, SCALAR_SHARE[0], P))
         quantize_w1(0)
         idle_bank = psum.tile([P, 512], F32, name="y_bank", bufs=Y_BANKS)
         for turn_number in range(WARM_PASSES):
@@ -132,7 +144,7 @@ def tile_picked_zres_gelu_po_kernel(
             w2_plane_raw[:].rearrange("p (m t) -> p t m", t=PACK),
         )
         quantize_w1(1)
-        last_picked = keep.tile([P, S - GATHER], U32, name="last_picked", tag="staged1", align_bytes=64)
+        last_picked = shared.tile([P, S - GATHER], U32, name="last_picked", align_bytes=64, offset=2048)
 
         out_codes = keep.tile([P, S], U32, name="out_codes", align_bytes=64)
         out_plane = keep.tile([P, S], U8, name="out_plane", align_bytes=64)

@@ -23,14 +23,14 @@ PASSES = K // (P * PACK)
 QUADS = 4
 BLOCK = 128
 GATHER = 256
-CHUNKS = (256, 256, 256, 128, 128)
+SCALAR_SHARE = 80
+CHUNKS = (128, 256, 256, 256, 128)
 H_ON_VECTOR = (0,)
 CAST_ON_SCALAR = (2, 3)
-H_BANKS = 4
-Y_BANKS = 4
-WARM_PASSES = 4
+H_BANKS = 5
+Y_BANKS = 3
+OPEN_BLOCKS = 3
 CODE_STORES = {1: 0, 3: 2, 4: 4}
-SCALAR_SHARE = (128, 64)
 
 
 def tile_picked_zres_gelu_po_kernel(
@@ -65,14 +65,13 @@ def tile_picked_zres_gelu_po_kernel(
             words = x_words[a].rearrange("p n t -> p (n t)").bitcast(I32)
             nc.sync.dma_start(x_table[a][:, n0:n1].bitcast(I32), words[:, n0:n1])
 
-        nc.sync.dma_start(offsets[:], offs)
-        nc.sync.dma_start(w2_raw[:].bitcast(I32), w2_words[0].bitcast(I32))
         def load_x_scales(r):
             for a in range(PASSES):
                 nc.sync.dma_start(
                     x_plane[4 * a + r : P : 32, :].bitcast(I32), x_scales[a, r : 16 : 4, :].bitcast(I32)
                 )
 
+        nc.sync.dma_start(offsets[:], offs)
         load_x(0, 0, T // 2)
         load_x_scales(0)
         load_x_scales(1)
@@ -87,10 +86,11 @@ def tile_picked_zres_gelu_po_kernel(
                 w2_plane_raw[32 * q : 32 * q + 4, :].bitcast(I32), w2_scales[0, 4 * q : 4 * q + 4, :].bitcast(I32)
             )
         load_x(1, 0, T)
+        nc.sync.dma_start(w2_raw[:].bitcast(I32), w2_words[0].bitcast(I32))
         nc.sync.dma_start(factor[:], turn.rearrange("(p t) o -> p (t o)", t=PACK))
 
         w1_bf = [
-            keep.tile([P, H * PACK], BF16, name="w1_bf0", align_bytes=64),
+            shared.tile([P, H * PACK], BF16, name="w1_bf0", align_bytes=64, offset=6144),
             shared.tile([P, H * PACK], BF16, name="w1_bf1", align_bytes=64, offset=2048),
         ]
         w1_codes = [
@@ -104,12 +104,9 @@ def tile_picked_zres_gelu_po_kernel(
         w2_plane = keep.tile([P, H], U8, name="w2_plane", align_bytes=64)
 
         def w1_views(a, m0, m1):
-            dst = w1_bf[a][:].rearrange("p (t m j) -> p m j t", t=PACK, j=PACK)[:, m0:m1]
-            src = w1_raw[a][:].rearrange("p j (m t) -> p m j t", t=PACK)[:, m0:m1]
-            return dst, src
-
-        def quantize_w1(a):
-            nc.vector.quantize_mx(w1_codes[a][:].bitcast(FP8X4), w1_plane[a][:], w1_bf[a][:])
+            dst = w1_bf[a][:].rearrange("p (t m j) -> p m j t", t=PACK, j=PACK)
+            src = w1_raw[a][:].rearrange("p j (m t) -> p m j t", t=PACK)
+            return dst[:, m0:m1], src[:, m0:m1]
 
         def gather_x(a, n0, picked):
             n1 = n0 + picked.shape[1]
@@ -117,34 +114,48 @@ def tile_picked_zres_gelu_po_kernel(
             for n in range(n0, n1, BLOCK):
                 x_picked[a, n] = picked[:, n - n0 : n - n0 + BLOCK]
 
-        nc.vector.tensor_copy(
-            w2_codes[:].rearrange("p (t m b) -> p t m b", t=PACK, b=2),
-            w2_raw[:].rearrange("p (m t b) -> p t m b", t=PACK, b=2),
-        )
         first_picked = keep.tile([P, S], U32, name="first_picked", align_bytes=64)
         gather_x(0, 0, first_picked[:])
         nc.vector.tensor_copy(x_picked_plane[:], x_plane[:].indirect(offsets[:]))
-        nc.scalar.copy(*w1_views(0, 0, SCALAR_SHARE[0]))
-        quantize_w1(0)
-        idle_bank = psum.tile([P, 512], F32, name="y_bank", bufs=Y_BANKS)
-        for turn_number in range(WARM_PASSES):
+        nc.scalar.copy(*w1_views(0, 0, P))
+        nc.vector.quantize_mx(w1_codes[0][:].bitcast(FP8X4), w1_plane[0][:], w1_bf[0][:])
+
+        h_banks = {}
+
+        def product_pass(n0, a, t, opens, closes):
             nc.tensor.matmul_mx(
-                idle_bank[:],
-                lhsT=w1_codes[0][:, 0:P].bitcast(FP8X4),
-                lhsT_scale=w1_plane[0][:, 0:P],
-                rhs=first_picked[:, 0:512].bitcast(FP8X4),
-                rhs_scale=x_picked_plane[:, 0:512],
-                start=True,
-                stop=True,
+                h_banks[n0][:, t, :],
+                lhsT=w1_codes[a][:, t * P : (t + 1) * P].bitcast(FP8X4),
+                lhsT_scale=w1_plane[a][:, t * P : (t + 1) * P],
+                rhs=x_picked[a, n0].bitcast(FP8X4),
+                rhs_scale=x_picked_plane[4 * a : P, n0 : n0 + BLOCK],
+                start=(opens and t == 0),
+                stop=(closes and t == PACK - 1),
             )
-        nc.scalar.copy(*w1_views(1, 0, SCALAR_SHARE[1]))
-        nc.vector.tensor_copy(*w1_views(1, SCALAR_SHARE[1], P))
+
+        def open_block(n0, a):
+            h_banks[n0] = psum.tile([P, PACK, BLOCK], F32, name="h_bank", bufs=H_BANKS)
+            for t in range(PACK):
+                product_pass(n0, a, t, True, False)
+
+        for n0 in range(0, OPEN_BLOCKS * BLOCK, BLOCK):
+            open_block(n0, 0)
+
+        nc.scalar.copy(*w1_views(1, 0, SCALAR_SHARE))
+        nc.vector.tensor_copy(*w1_views(1, SCALAR_SHARE, P))
         nc.vector.tensor_copy(
             w2_plane[:].rearrange("p (t m) -> p t m", t=PACK),
             w2_plane_raw[:].rearrange("p (m t) -> p t m", t=PACK),
         )
-        quantize_w1(1)
-        last_picked = shared.tile([P, S - GATHER], U32, name="last_picked", align_bytes=64, offset=2048)
+        nc.vector.quantize_mx(w1_codes[1][:].bitcast(FP8X4), w1_plane[1][:], w1_bf[1][:])
+        last_picked = shared.tile([P, S], U32, name="last_picked", align_bytes=64, offset=2048)
+        for n0 in range(0, S, GATHER):
+            gather_x(1, n0, last_picked[:, n0 : n0 + GATHER])
+
+        nc.scalar.copy(
+            w2_codes[:].bitcast(U16).rearrange("p (t m) -> p m t", t=PACK),
+            w2_raw[:].bitcast(U16).rearrange("p (m t) -> p m t", t=PACK),
+        )
 
         out_codes = keep.tile([P, S], U32, name="out_codes", align_bytes=64)
         out_plane = keep.tile([P, S], U8, name="out_plane", align_bytes=64)
@@ -162,37 +173,27 @@ def tile_picked_zres_gelu_po_kernel(
         result_bf = [keep.tile([P, w * PACK], BF16, name="result_bf%d" % c, align_bytes=64) for c, w in enumerate(CHUNKS)]
 
         def project(c):
-            banks = []
-            for n0 in range(starts[c], starts[c] + CHUNKS[c], BLOCK):
-                if n0 == S - GATHER:
-                    tail_picked = keep.tile([P, GATHER], U32, name="tail_picked", tag="g_bf0", align_bytes=64)
-                    gather_x(1, n0, tail_picked[:])
-                elif n0 % GATHER == 0:
-                    gather_x(1, n0, last_picked[:, n0 : n0 + GATHER])
-                bank = psum.tile([P, PACK, BLOCK], F32, name="h_bank", bufs=H_BANKS)
+            blocks = range(starts[c], starts[c] + CHUNKS[c], BLOCK)
+            for n0 in blocks:
+                closing = 1 if n0 in h_banks else 0
+                if n0 not in h_banks:
+                    open_block(n0, 1)
                 for t in range(PACK):
-                    for a in range(PASSES):
-                        nc.tensor.matmul_mx(
-                            bank[:, t, :],
-                            lhsT=w1_codes[a][:, t * P : (t + 1) * P].bitcast(FP8X4),
-                            lhsT_scale=w1_plane[a][:, t * P : (t + 1) * P],
-                            rhs=x_picked[a, n0].bitcast(FP8X4),
-                            rhs_scale=x_picked_plane[4 * a : P, n0 : n0 + BLOCK],
-                            start=(a == 0),
-                            stop=(a == PASSES - 1),
-                        )
+                    product_pass(n0, closing, t, False, True)
                 local = n0 - starts[c]
                 nc.scalar.activation(
                     g_bf[c][:, local * PACK : (local + BLOCK) * PACK].rearrange("p (n t) -> p n t", t=PACK),
-                    bank[:].rearrange("p t n -> p n t"),
+                    h_banks[n0][:].rearrange("p t n -> p n t"),
                     GELU,
                 )
-                banks.append((n0, local, bank))
-            for n0, local, bank in banks:
+
+        def keep_h(c):
+            for n0 in range(starts[c], starts[c] + CHUNKS[c], BLOCK):
+                local = n0 - starts[c]
                 if n0 // BLOCK in H_ON_VECTOR:
-                    nc.vector.tensor_copy(h_kept[c][:, :, local : local + BLOCK], bank[:])
+                    nc.vector.tensor_copy(h_kept[c][:, :, local : local + BLOCK], h_banks[n0][:])
                 else:
-                    nc.scalar.copy(h_kept[c][:, :, local : local + BLOCK], bank[:])
+                    nc.scalar.copy(h_kept[c][:, :, local : local + BLOCK], h_banks[n0][:])
 
         def quantize_g(c):
             nc.vector.quantize_mx(g_codes[c][:].bitcast(FP8X4), g_plane[c][:], g_bf[c][:])
@@ -242,11 +243,11 @@ def tile_picked_zres_gelu_po_kernel(
                 cols = slice(starts[CODE_STORES[c]], cols.stop)
                 nc.sync.dma_start(out_words[:, cols], out_codes[:, cols].bitcast(I32))
 
-        stages = (project, quantize_g, branch, round_result, quantize_result)
-        for step in range(len(CHUNKS) + len(stages) - 1):
-            for s, stage in reversed(list(enumerate(stages))):
-                if 0 <= step - s < len(CHUNKS):
-                    stage(step - s)
+        lags = ((quantize_result, 4), (round_result, 3), (branch, 2), (quantize_g, 1), (project, 0), (keep_h, 1))
+        for step in range(len(CHUNKS) + 4):
+            for stage, lag in lags:
+                if 0 <= step - lag < len(CHUNKS):
+                    stage(step - lag)
 
         for q in range(QUADS):
             queue = nc.sync if q % 2 == 0 else nc.scalar

@@ -25,11 +25,11 @@ BLOCK = 128
 GATHER = 256
 SCALAR_SHARE = 80
 CHUNKS = (128, 256, 256, 256, 128)
-H_ON_VECTOR = (0,)
+H_ON_VECTOR = (0, 1)
 CAST_ON_SCALAR = (2, 3)
 H_BANKS = 5
 Y_BANKS = 3
-OPEN_BLOCKS = 3
+OPEN_BLOCKS = 4
 CODE_STORES = {1: 0, 3: 2, 4: 4}
 
 
@@ -44,7 +44,7 @@ def tile_picked_zres_gelu_po_kernel(
 
         offsets = keep.tile([P, S // 16], U16, name="offsets")
         x_plane = shared.tile([P, T], U8, name="x_plane", align_bytes=64, offset=1024)
-        w2_plane_raw = keep.tile([P, H], U8, name="w2_plane_raw", align_bytes=64)
+        w2_plane_raw = shared.tile([P, H], U8, name="w2_plane_raw", align_bytes=64, offset=10240)
         warm = keep.tile([P, 8], F32, name="warm")
         warm_out = keep.tile([P, 8], F32, name="warm_out")
         nc.vector.memset(x_plane[:].bitcast(I32), 0)
@@ -71,8 +71,8 @@ def tile_picked_zres_gelu_po_kernel(
                     x_plane[4 * a + r : P : 32, :].bitcast(I32), x_scales[a, r : 16 : 4, :].bitcast(I32)
                 )
 
-        nc.sync.dma_start(offsets[:], offs)
         load_x(0, 0, T // 2)
+        nc.sync.dma_start(offsets[:], offs)
         load_x_scales(0)
         load_x_scales(1)
         load_x(0, T // 2, T)
@@ -95,7 +95,7 @@ def tile_picked_zres_gelu_po_kernel(
         ]
         w1_codes = [
             shared.tile([P, H], U32, name="w1_codes0", align_bytes=64, offset=0),
-            keep.tile([P, H], U32, name="w1_codes1", align_bytes=64),
+            shared.tile([P, H], U32, name="w1_codes1", align_bytes=64, offset=10240),
         ]
         w1_plane = [keep.tile([P, H], U8, name="w1_plane%d" % a, align_bytes=64) for a in range(PASSES)]
         x_picked = {}

@@ -222,7 +222,8 @@ def tile_picked_zres_gelu_po_kernel(
                         MULT,
                         ADD,
                     )
-            nc.sync.dma_start(out_rows[:, :, starts[c] : starts[c] + w], result[c][:])
+                quarters = slice(t0, t0 + per_bank)
+                nc.sync.dma_start(out_rows[:, quarters, starts[c] : starts[c] + w], result[c][:, quarters, :])
 
         def round_result(c):
             dst = result_bf[c][:].rearrange("p (n i t) -> p n t i", i=4, t=PACK)
@@ -243,8 +244,8 @@ def tile_picked_zres_gelu_po_kernel(
                 cols = slice(starts[CODE_STORES[c]], cols.stop)
                 nc.sync.dma_start(out_words[:, cols], out_codes[:, cols].bitcast(I32))
 
-        lags = ((quantize_result, 4), (round_result, 3), (branch, 2), (quantize_g, 1), (project, 0), (keep_h, 1))
-        for step in range(len(CHUNKS) + 4):
+        lags = ((quantize_g, 1), (branch, 2), (quantize_result, 5), (round_result, 4), (project, 0), (keep_h, 0))
+        for step in range(len(CHUNKS) + 5):
             for stage, lag in lags:
                 if 0 <= step - lag < len(CHUNKS):
                     stage(step - lag)

@@ -23,7 +23,8 @@ PASSES = K // (P * PACK)
 QUADS = 4
 BLOCK = 128
 GATHER = 256
-SCALAR_SHARE = 80
+SCALAR_SHARE = 64
+FIRST_PIECE = 3 * T // 8
 CHUNKS = (128, 256, 256, 256, 128)
 H_ON_VECTOR = (0, 1)
 CAST_ON_SCALAR = (2, 3)
@@ -43,65 +44,70 @@ def tile_picked_zres_gelu_po_kernel(
         psum = ctx.enter_context(tc.psum_pool(name="psum", bufs=4))
 
         offsets = keep.tile([P, S // 16], U16, name="offsets")
-        x_plane = shared.tile([P, T], U8, name="x_plane", align_bytes=64, offset=1024)
-        w2_plane_raw = shared.tile([P, H], U8, name="w2_plane_raw", align_bytes=64, offset=10240)
+        x_rows = shared.tile([P, T], U8, name="x_rows", align_bytes=64, offset=0)
+        w2_rows = keep.tile([P, H], U8, name="w2_rows", align_bytes=64)
         warm = keep.tile([P, 8], F32, name="warm")
         warm_out = keep.tile([P, 8], F32, name="warm_out")
-        nc.vector.memset(x_plane[:].bitcast(I32), 0)
-        nc.vector.memset(w2_plane_raw[:].bitcast(I32), 0)
+        nc.vector.memset(x_rows[:].bitcast(I32), 0)
+        nc.vector.memset(w2_rows[:].bitcast(I32), 0)
         nc.vector.memset(warm[:], 0.0)
         nc.scalar.activation(warm_out[:], warm[:], GELU)
 
+        held = 4096 + 4 * T
+        picked_rows = shared.tile([P, S], U8, name="picked_rows", align_bytes=64, offset=held - 128)
         w1_raw = [keep.tile([P, PACK, H], F32, name="w1_raw%d" % a) for a in range(PASSES)]
-        x_table = [keep.tile([P, T], U32, name="x_table%d" % a, align_bytes=64) for a in range(PASSES)]
-        w2_raw = keep.tile([P, 2 * H], U8, name="w2_raw", align_bytes=64)
-        factor = keep.tile([P, PACK], F32, name="factor")
+        x_table = [
+            keep.tile([P, T], U32, name="x_table0", align_bytes=64),
+            shared.tile([P, T], U32, name="x_table1", align_bytes=64, offset=4096),
+        ]
+        factor = shared.tile([P, PACK], F32, name="factor", align_bytes=64, offset=held)
+        w2_plane = shared.tile([P, H], U8, name="w2_plane", align_bytes=64, offset=held + 64)
+        w2_raw = shared.tile([P, 2 * H], U8, name="w2_raw", align_bytes=64, offset=held + 64 + H)
+        x_picked_plane = keep.tile([P, S], U8, name="x_picked_plane", align_bytes=64)
 
-        def load_w1(a, j0, j1):
+        def load_w1(a):
             rows = w1[a * 512 : (a + 1) * 512, :].rearrange("(p j) c -> p j c", j=PACK)
-            nc.sync.dma_start(w1_raw[a][:, j0:j1, :], rows[:, j0:j1, :])
+            nc.sync.dma_start(w1_raw[a][:], rows)
 
         def load_x(a, n0, n1):
             words = x_words[a].rearrange("p n t -> p (n t)").bitcast(I32)
             nc.sync.dma_start(x_table[a][:, n0:n1].bitcast(I32), words[:, n0:n1])
 
-        def load_x_scales(r):
-            for a in range(PASSES):
+        def gather_rows(plane, first):
+            for r in range(1, 4):
                 nc.sync.dma_start(
-                    x_plane[4 * a + r : P : 32, :].bitcast(I32), x_scales[a, r : 16 : 4, :].bitcast(I32)
+                    plane[first + r : P : 32, :].bitcast(I32), plane[first + 8 * r : P : 32, :].bitcast(I32)
                 )
 
-        load_x(0, 0, T // 2)
+        load_x(0, 0, FIRST_PIECE)
         nc.sync.dma_start(offsets[:], offs)
-        load_x_scales(0)
-        load_x_scales(1)
-        load_x(0, T // 2, T)
-        load_w1(0, 0, 2)
-        load_x_scales(2)
-        load_x_scales(3)
-        load_w1(0, 2, PACK)
-        load_w1(1, 0, PACK)
-        for q in range(QUADS):
-            nc.sync.dma_start(
-                w2_plane_raw[32 * q : 32 * q + 4, :].bitcast(I32), w2_scales[0, 4 * q : 4 * q + 4, :].bitcast(I32)
-            )
+        for a in range(PASSES):
+            nc.sync.dma_start(x_rows[4 * a : P : 8, :].bitcast(I32), x_scales[a].bitcast(I32))
+        nc.sync.dma_start(w2_rows[0:P:8, :].bitcast(I32), w2_scales[0].bitcast(I32))
+        load_x(0, FIRST_PIECE, T)
+        load_w1(0)
+        load_w1(1)
+        nc.vector.tensor_copy(picked_rows[:], x_rows[:].indirect(offsets[:]))
+        nc.vector.tensor_copy(x_picked_plane[:].bitcast(I32), picked_rows[:].bitcast(I32))
+        for a in range(PASSES):
+            gather_rows(x_picked_plane, 4 * a)
         load_x(1, 0, T)
         nc.sync.dma_start(w2_raw[:].bitcast(I32), w2_words[0].bitcast(I32))
         nc.sync.dma_start(factor[:], turn.rearrange("(p t) o -> p (t o)", t=PACK))
+        nc.vector.tensor_copy(
+            w2_plane[:].rearrange("p (t m) -> p t m", t=PACK),
+            w2_rows[:].rearrange("p (m t) -> p t m", t=PACK),
+        )
+        gather_rows(w2_plane, 0)
 
         w1_bf = [
-            shared.tile([P, H * PACK], BF16, name="w1_bf0", align_bytes=64, offset=6144),
-            shared.tile([P, H * PACK], BF16, name="w1_bf1", align_bytes=64, offset=2048),
+            keep.tile([P, H * PACK], BF16, name="w1_bf0", align_bytes=64),
+            shared.tile([P, H * PACK], BF16, name="w1_bf1", align_bytes=64, offset=held + 2048),
         ]
-        w1_codes = [
-            shared.tile([P, H], U32, name="w1_codes0", align_bytes=64, offset=0),
-            shared.tile([P, H], U32, name="w1_codes1", align_bytes=64, offset=10240),
-        ]
+        w1_codes = [keep.tile([P, H], U32, name="w1_codes%d" % a, align_bytes=64) for a in range(PASSES)]
         w1_plane = [keep.tile([P, H], U8, name="w1_plane%d" % a, align_bytes=64) for a in range(PASSES)]
         x_picked = {}
-        x_picked_plane = keep.tile([P, S], U8, name="x_picked_plane", align_bytes=64)
         w2_codes = keep.tile([P, 2 * H], U8, name="w2_codes", align_bytes=64)
-        w2_plane = keep.tile([P, H], U8, name="w2_plane", align_bytes=64)
 
         def w1_views(a, m0, m1):
             dst = w1_bf[a][:].rearrange("p (t m j) -> p m j t", t=PACK, j=PACK)
@@ -114,9 +120,8 @@ def tile_picked_zres_gelu_po_kernel(
             for n in range(n0, n1, BLOCK):
                 x_picked[a, n] = picked[:, n - n0 : n - n0 + BLOCK]
 
-        first_picked = keep.tile([P, S], U32, name="first_picked", align_bytes=64)
+        first_picked = shared.tile([P, S], U32, name="first_picked", align_bytes=64, offset=0)
         gather_x(0, 0, first_picked[:])
-        nc.vector.tensor_copy(x_picked_plane[:], x_plane[:].indirect(offsets[:]))
         nc.scalar.copy(*w1_views(0, 0, P))
         nc.vector.quantize_mx(w1_codes[0][:].bitcast(FP8X4), w1_plane[0][:], w1_bf[0][:])
 
@@ -143,12 +148,8 @@ def tile_picked_zres_gelu_po_kernel(
 
         nc.scalar.copy(*w1_views(1, 0, SCALAR_SHARE))
         nc.vector.tensor_copy(*w1_views(1, SCALAR_SHARE, P))
-        nc.vector.tensor_copy(
-            w2_plane[:].rearrange("p (t m) -> p t m", t=PACK),
-            w2_plane_raw[:].rearrange("p (m t) -> p t m", t=PACK),
-        )
         nc.vector.quantize_mx(w1_codes[1][:].bitcast(FP8X4), w1_plane[1][:], w1_bf[1][:])
-        last_picked = shared.tile([P, S], U32, name="last_picked", align_bytes=64, offset=2048)
+        last_picked = shared.tile([P, S], U32, name="last_picked", align_bytes=64, offset=held + 2048)
         for n0 in range(0, S, GATHER):
             gather_x(1, n0, last_picked[:, n0 : n0 + GATHER])
 

@@ -1,6 +1,7 @@
 from contextlib import ExitStack
 
 import concourse.mybir as mybir
+from concourse.masks import make_identity
 
 K, T, S, H = 1024, 2048, 1024, 512
 FLOPS = 2 * K * H * S + 2 * H * H * S
@@ -22,16 +23,18 @@ PACK = 4
 PASSES = K // (P * PACK)
 QUADS = 4
 BLOCK = 128
-GATHER = 256
+GATHERS = (128, 128, 256, 256)
 SCALAR_SHARE = 64
 FIRST_PIECE = 3 * T // 8
-CHUNKS = (128, 256, 256, 256, 128)
-H_ON_VECTOR = (0, 1)
-CAST_ON_SCALAR = (2, 3)
-H_BANKS = 5
+G_SPANS = ((0, 128), (128, 256), (384, 256), (640, 256), (896, 128))
+PIECES = ((0, 128), (128, 256), (384, 256), (640, 128), (768, 128), (896, 128))
+ROUNDED = G_SPANS
+H_ON_VECTOR = (0, 4)
+ROUND_ON_GPSIMD = (0, 128, 384)
+H_BANKS = 4
 Y_BANKS = 3
 OPEN_BLOCKS = 4
-CODE_STORES = {1: 0, 3: 2, 4: 4}
+CODE_STORES = {128: 0, 640: 384, 896: 896}
 
 
 def tile_picked_zres_gelu_po_kernel(
@@ -52,6 +55,11 @@ def tile_picked_zres_gelu_po_kernel(
         nc.vector.memset(w2_rows[:].bitcast(I32), 0)
         nc.vector.memset(warm[:], 0.0)
         nc.scalar.activation(warm_out[:], warm[:], GELU)
+        identity = keep.tile([P, P], F32, name="identity")
+        turn_row = keep.tile([P, H], F32, name="turn_row")
+        nc.vector.memset(turn_row[:], 0.0)
+        nc.vector.memset(identity[:], 0.0)
+        make_identity(nc, identity[:], nomemset=True)
 
         held = 4096 + 4 * T
         picked_rows = shared.tile([P, S], U8, name="picked_rows", align_bytes=64, offset=held - 128)
@@ -60,7 +68,6 @@ def tile_picked_zres_gelu_po_kernel(
             keep.tile([P, T], U32, name="x_table0", align_bytes=64),
             shared.tile([P, T], U32, name="x_table1", align_bytes=64, offset=4096),
         ]
-        factor = shared.tile([P, PACK], F32, name="factor", align_bytes=64, offset=held)
         w2_plane = shared.tile([P, H], U8, name="w2_plane", align_bytes=64, offset=held + 64)
         w2_raw = shared.tile([P, 2 * H], U8, name="w2_raw", align_bytes=64, offset=held + 64 + H)
         x_picked_plane = keep.tile([P, S], U8, name="x_picked_plane", align_bytes=64)
@@ -85,6 +92,7 @@ def tile_picked_zres_gelu_po_kernel(
             nc.sync.dma_start(x_rows[4 * a : P : 8, :].bitcast(I32), x_scales[a].bitcast(I32))
         nc.sync.dma_start(w2_rows[0:P:8, :].bitcast(I32), w2_scales[0].bitcast(I32))
         load_x(0, FIRST_PIECE, T)
+        nc.sync.dma_start(turn_row[0:1, :], turn.rearrange("m o -> o m"))
         load_w1(0)
         load_w1(1)
         nc.vector.tensor_copy(picked_rows[:], x_rows[:].indirect(offsets[:]))
@@ -93,7 +101,9 @@ def tile_picked_zres_gelu_po_kernel(
             gather_rows(x_picked_plane, 4 * a)
         load_x(1, 0, T)
         nc.sync.dma_start(w2_raw[:].bitcast(I32), w2_words[0].bitcast(I32))
-        nc.sync.dma_start(factor[:], turn.rearrange("(p t) o -> p (t o)", t=PACK))
+        factor = psum.tile([P, PACK, P], F32, name="factor", bufs=1)
+        for t in range(PACK):
+            nc.tensor.transpose(factor[:, t, :], turn_row[:, t:H:PACK], identity[:])
         nc.vector.tensor_copy(
             w2_plane[:].rearrange("p (t m) -> p t m", t=PACK),
             w2_rows[:].rearrange("p (m t) -> p t m", t=PACK),
@@ -149,9 +159,10 @@ def tile_picked_zres_gelu_po_kernel(
         nc.scalar.copy(*w1_views(1, 0, SCALAR_SHARE))
         nc.vector.tensor_copy(*w1_views(1, SCALAR_SHARE, P))
         nc.vector.quantize_mx(w1_codes[1][:].bitcast(FP8X4), w1_plane[1][:], w1_bf[1][:])
-        last_picked = shared.tile([P, S], U32, name="last_picked", align_bytes=64, offset=held + 2048)
-        for n0 in range(0, S, GATHER):
-            gather_x(1, n0, last_picked[:, n0 : n0 + GATHER])
+        last_picked = shared.tile([P, sum(GATHERS)], U32, name="last_picked", align_bytes=64, offset=held + 2048)
+        for i, width in enumerate(GATHERS):
+            n0 = sum(GATHERS[:i])
+            gather_x(1, n0, last_picked[:, n0 : n0 + width])
 
         nc.scalar.copy(
             w2_codes[:].bitcast(U16).rearrange("p (t m) -> p m t", t=PACK),
@@ -163,44 +174,61 @@ def tile_picked_zres_gelu_po_kernel(
         out_rows = out_0.rearrange("(p t) n -> p t n", t=PACK)
         out_words = out_1[0].rearrange("p n t -> p (n t)").bitcast(I32)
 
-        starts = [sum(CHUNKS[:c]) for c in range(len(CHUNKS))]
-        h_kept = [keep.tile([P, PACK, w], F32, name="h_kept%d" % c) for c, w in enumerate(CHUNKS)]
-        g_bf = [
-            keep.tile([P, w * PACK], BF16, name="g_bf", tag="g_bf%d" % c, align_bytes=64) for c, w in enumerate(CHUNKS)
-        ]
-        g_codes = [keep.tile([P, w], U32, name="g_codes%d" % c, align_bytes=64) for c, w in enumerate(CHUNKS)]
-        g_plane = [keep.tile([P, w], U8, name="g_plane%d" % c, align_bytes=64) for c, w in enumerate(CHUNKS)]
-        result = [keep.tile([P, PACK, w], F32, name="result%d" % c) for c, w in enumerate(CHUNKS)]
-        result_bf = [keep.tile([P, w * PACK], BF16, name="result_bf%d" % c, align_bytes=64) for c, w in enumerate(CHUNKS)]
-
-        def project(c):
-            blocks = range(starts[c], starts[c] + CHUNKS[c], BLOCK)
-            for n0 in blocks:
-                closing = 1 if n0 in h_banks else 0
-                if n0 not in h_banks:
-                    open_block(n0, 1)
-                for t in range(PACK):
-                    product_pass(n0, closing, t, False, True)
-                local = n0 - starts[c]
-                nc.scalar.activation(
-                    g_bf[c][:, local * PACK : (local + BLOCK) * PACK].rearrange("p (n t) -> p n t", t=PACK),
-                    h_banks[n0][:].rearrange("p t n -> p n t"),
-                    GELU,
+        def tiles(pool, name, dtype, per_token, spans, at=None):
+            return {
+                n0: pool.tile(
+                    [P, w * per_token], dtype, name="%s%d" % (name, n0), align_bytes=64,
+                    **({} if at is None else {"offset": at[n0]})
                 )
+                for n0, w in spans
+            }
 
-        def keep_h(c):
-            for n0 in range(starts[c], starts[c] + CHUNKS[c], BLOCK):
-                local = n0 - starts[c]
-                if n0 // BLOCK in H_ON_VECTOR:
-                    nc.vector.tensor_copy(h_kept[c][:, :, local : local + BLOCK], h_banks[n0][:])
-                else:
-                    nc.scalar.copy(h_kept[c][:, :, local : local + BLOCK], h_banks[n0][:])
+        def span_of(spans, n):
+            return max(span for span in spans if span[0] <= n)
 
-        def quantize_g(c):
-            nc.vector.quantize_mx(g_codes[c][:].bitcast(FP8X4), g_plane[c][:], g_bf[c][:])
+        ring = held + 8192
+        g_bf = tiles(shared, "g_bf", BF16, PACK, G_SPANS, {0: ring, 128: ring + 1024, 384: ring + 3072, 640: ring + 5120, 896: 2048 + ring + 7168})
+        late_picked = shared.tile([P, S - sum(GATHERS)], U32, name="late_picked", align_bytes=64, offset=ring + 1024)
+        g_codes = tiles(keep, "g_codes", U32, 1, G_SPANS)
+        g_plane = tiles(keep, "g_plane", U8, 1, G_SPANS)
+        h_kept = tiles(keep, "h_kept", F32, PACK, PIECES)
+        result = tiles(keep, "result", F32, PACK, PIECES)
+        result_bf = tiles(shared, "result_bf", BF16, PACK, ROUNDED, {0: 4096, 128: 4096, 384: ring + 7168 + 1024, 640: 8192, 896: 10240})
 
-        def branch(c):
-            w = CHUNKS[c]
+        def quarters_of(tile):
+            return tile[:].rearrange("p (t n) -> p t n", t=PACK)
+
+        def project(b):
+            n0 = b * BLOCK
+            closing = 1 if n0 in h_banks else 0
+            if n0 not in h_banks:
+                open_block(n0, 1)
+            for t in range(PACK):
+                product_pass(n0, closing, t, False, True)
+            first = span_of(G_SPANS, n0)[0]
+            local = n0 - first
+            nc.scalar.activation(
+                g_bf[first][:, local * PACK : (local + BLOCK) * PACK].rearrange("p (n t) -> p n t", t=PACK),
+                h_banks[n0][:].rearrange("p t n -> p n t"),
+                GELU,
+            )
+
+        def keep_h(b):
+            n0 = b * BLOCK
+            first = span_of(PIECES, n0)[0]
+            dst = quarters_of(h_kept[first])[:, :, n0 - first : n0 - first + BLOCK]
+            if b in H_ON_VECTOR:
+                nc.vector.tensor_copy(dst, h_banks[n0][:])
+            else:
+                nc.scalar.copy(dst, h_banks[n0][:])
+
+        def quantize_g(n0):
+            nc.vector.quantize_mx(g_codes[n0][:].bitcast(FP8X4), g_plane[n0][:], g_bf[n0][:])
+
+        def branch(n0):
+            w = span_of(PIECES, n0)[1]
+            first = span_of(G_SPANS, n0)[0]
+            cols = slice(n0 - first, n0 - first + w)
             per_bank = 512 // w
             for t0 in range(0, PACK, per_bank):
                 bank = psum.tile([P, 512], F32, name="y_bank", bufs=Y_BANKS)
@@ -209,47 +237,86 @@ def tile_picked_zres_gelu_po_kernel(
                         bank[:, (t - t0) * w : (t - t0 + 1) * w],
                         lhsT=w2_codes[:, t * 2 * P : (t + 1) * 2 * P].bitcast(FP4X4),
                         lhsT_scale=w2_plane[:, t * P : (t + 1) * P],
-                        rhs=g_codes[c][:].bitcast(FP8X4),
-                        rhs_scale=g_plane[c][:],
+                        rhs=g_codes[first][:, cols].bitcast(FP8X4),
+                        rhs_scale=g_plane[first][:, cols],
                         start=True,
                         stop=True,
                     )
                 for t in range(t0, t0 + per_bank):
                     nc.vector.scalar_tensor_tensor(
-                        result[c][:, t, :],
+                        quarters_of(result[n0])[:, t, :],
                         bank[:, (t - t0) * w : (t - t0 + 1) * w],
-                        factor[:, t : t + 1],
-                        h_kept[c][:, t, :],
+                        factor[:, t, 0:1],
+                        quarters_of(h_kept[n0])[:, t, :],
                         MULT,
                         ADD,
                     )
                 quarters = slice(t0, t0 + per_bank)
-                nc.sync.dma_start(out_rows[:, quarters, starts[c] : starts[c] + w], result[c][:, quarters, :])
+                nc.sync.dma_start(out_rows[:, quarters, n0 : n0 + w], quarters_of(result[n0])[:, quarters, :])
 
-        def round_result(c):
-            dst = result_bf[c][:].rearrange("p (n i t) -> p n t i", i=4, t=PACK)
-            src = result[c][:].rearrange("p t (n i) -> p n t i", i=4)
-            if c == len(CHUNKS) - 1:
-                half = CHUNKS[c] // 8
-                nc.scalar.copy(dst[:, :half], src[:, :half])
-                nc.vector.tensor_copy(dst[:, half:], src[:, half:])
-            elif c in CAST_ON_SCALAR:
-                nc.scalar.copy(dst, src)
+        def round_result(n0):
+            w = span_of(PIECES, n0)[1]
+            first = span_of(ROUNDED, n0)[0]
+            out = result_bf[first][:, (n0 - first) * PACK : (n0 - first + w) * PACK]
+            if n0 in ROUND_ON_GPSIMD:
+                nc.gpsimd.tensor_scalar(
+                    out.rearrange("p (n t) -> p n t", t=PACK),
+                    result[n0][:].rearrange("p (t n) -> p n t", t=PACK),
+                    1.0,
+                    0.0,
+                    MULT,
+                    ADD,
+                )
             else:
-                nc.vector.tensor_copy(dst, src)
+                nc.scalar.copy(
+                    out.rearrange("p (n i t) -> p n t i", i=4, t=PACK),
+                    result[n0][:].rearrange("p (t n i) -> p n t i", i=4, t=PACK),
+                )
 
-        def quantize_result(c):
-            cols = slice(starts[c], starts[c] + CHUNKS[c])
-            nc.vector.quantize_mx(out_codes[:, cols].bitcast(FP8X4), out_plane[:, cols], result_bf[c][:])
-            if c in CODE_STORES:
-                cols = slice(starts[CODE_STORES[c]], cols.stop)
+        def quantize_result(n0):
+            cols = slice(n0, n0 + span_of(ROUNDED, n0)[1])
+            nc.vector.quantize_mx(out_codes[:, cols].bitcast(FP8X4), out_plane[:, cols], result_bf[n0][:])
+            if n0 in CODE_STORES:
+                cols = slice(CODE_STORES[n0], cols.stop)
                 nc.sync.dma_start(out_words[:, cols], out_codes[:, cols].bitcast(I32))
 
-        lags = ((quantize_g, 1), (branch, 2), (quantize_result, 5), (round_result, 4), (project, 0), (keep_h, 0))
-        for step in range(len(CHUNKS) + 5):
-            for stage, lag in lags:
-                if 0 <= step - lag < len(CHUNKS):
-                    stage(step - lag)
+        project(0)
+        project(1)
+        quantize_g(0)
+        keep_h(0)
+        branch(0)
+        project(2)
+        keep_h(1)
+        quantize_g(128)
+        gather_x(1, sum(GATHERS), late_picked[:])
+        round_result(0)
+        keep_h(2)
+        branch(128)
+        project(3)
+        project(4)
+        keep_h(3)
+        quantize_g(384)
+        quantize_result(0)
+        round_result(128)
+        keep_h(4)
+        branch(384)
+        project(5)
+        project(6)
+        keep_h(5)
+        project(7)
+        quantize_g(640)
+        quantize_result(128)
+        quantize_g(896)
+        round_result(384)
+        for b in range(5, 8):
+            if b > 5:
+                keep_h(b)
+            branch(b * BLOCK)
+        for b in range(5, 8):
+            round_result(b * BLOCK)
+        quantize_result(384)
+        quantize_result(640)
+        quantize_result(896)
 
         for q in range(QUADS):
             queue = nc.sync if q % 2 == 0 else nc.scalar

@@ -23,8 +23,8 @@ PACK = 4
 PASSES = K // (P * PACK)
 QUADS = 4
 BLOCK = 128
-GATHERS = (128, 128, 256, 256)
-SCALAR_SHARE = 64
+GATHERS = (128, 128, 256, 256, 256)
+SCALAR_SHARES = (100, 76)
 FIRST_PIECE = 3 * T // 8
 G_SPANS = ((0, 128), (128, 256), (384, 256), (640, 256), (896, 128))
 PIECES = ((0, 128), (128, 256), (384, 256), (640, 128), (768, 128), (896, 128))
@@ -33,7 +33,7 @@ H_ON_VECTOR = (0, 4)
 ROUND_ON_GPSIMD = (0, 128, 384)
 H_BANKS = 4
 Y_BANKS = 3
-OPEN_BLOCKS = 4
+OPEN_BLOCKS = 3
 CODE_STORES = {128: 0, 640: 384, 896: 896}
 
 
@@ -68,9 +68,8 @@ def tile_picked_zres_gelu_po_kernel(
             keep.tile([P, T], U32, name="x_table0", align_bytes=64),
             shared.tile([P, T], U32, name="x_table1", align_bytes=64, offset=4096),
         ]
-        w2_plane = shared.tile([P, H], U8, name="w2_plane", align_bytes=64, offset=held + 64)
-        w2_raw = shared.tile([P, 2 * H], U8, name="w2_raw", align_bytes=64, offset=held + 64 + H)
-        x_picked_plane = keep.tile([P, S], U8, name="x_picked_plane", align_bytes=64)
+        w2_raw = shared.tile([P, 2 * H], U8, name="w2_raw", align_bytes=64, offset=held + 64)
+        x_planes = [keep.tile([P, S], U8, name="x_plane%d" % a, align_bytes=64) for a in range(PASSES)]
 
         def load_w1(a):
             rows = w1[a * 512 : (a + 1) * 512, :].rearrange("(p j) c -> p j c", j=PACK)
@@ -96,26 +95,23 @@ def tile_picked_zres_gelu_po_kernel(
         load_w1(0)
         load_w1(1)
         nc.vector.tensor_copy(picked_rows[:], x_rows[:].indirect(offsets[:]))
-        nc.vector.tensor_copy(x_picked_plane[:].bitcast(I32), picked_rows[:].bitcast(I32))
         for a in range(PASSES):
-            gather_rows(x_picked_plane, 4 * a)
+            nc.vector.tensor_copy(x_planes[a][:].bitcast(I32), picked_rows[:].bitcast(I32))
+        gather_rows(x_planes[0], 0)
         load_x(1, 0, T)
         nc.sync.dma_start(w2_raw[:].bitcast(I32), w2_words[0].bitcast(I32))
+        gather_rows(x_planes[1], 4)
         factor = psum.tile([P, PACK, P], F32, name="factor", bufs=1)
         for t in range(PACK):
             nc.tensor.transpose(factor[:, t, :], turn_row[:, t:H:PACK], identity[:])
-        nc.vector.tensor_copy(
-            w2_plane[:].rearrange("p (t m) -> p t m", t=PACK),
-            w2_rows[:].rearrange("p (m t) -> p t m", t=PACK),
-        )
-        gather_rows(w2_plane, 0)
 
         w1_bf = [
-            keep.tile([P, H * PACK], BF16, name="w1_bf0", align_bytes=64),
+            shared.tile([P, H * PACK], BF16, name="w1_bf0", align_bytes=64, offset=held + 6144),
             shared.tile([P, H * PACK], BF16, name="w1_bf1", align_bytes=64, offset=held + 2048),
         ]
         w1_codes = [keep.tile([P, H], U32, name="w1_codes%d" % a, align_bytes=64) for a in range(PASSES)]
         w1_plane = [keep.tile([P, H], U8, name="w1_plane%d" % a, align_bytes=64) for a in range(PASSES)]
+        w2_plane = shared.tile([P, H], U8, name="w2_plane", align_bytes=64, offset=held + 6144)
         x_picked = {}
         w2_codes = keep.tile([P, 2 * H], U8, name="w2_codes", align_bytes=64)
 
@@ -132,8 +128,14 @@ def tile_picked_zres_gelu_po_kernel(
 
         first_picked = shared.tile([P, S], U32, name="first_picked", align_bytes=64, offset=0)
         gather_x(0, 0, first_picked[:])
-        nc.scalar.copy(*w1_views(0, 0, P))
+        nc.scalar.copy(*w1_views(0, 0, SCALAR_SHARES[0]))
+        nc.vector.tensor_copy(*w1_views(0, SCALAR_SHARES[0], P))
         nc.vector.quantize_mx(w1_codes[0][:].bitcast(FP8X4), w1_plane[0][:], w1_bf[0][:])
+        nc.vector.tensor_copy(
+            w2_plane[:].rearrange("p (t m) -> p t m", t=PACK),
+            w2_rows[:].rearrange("p (m t) -> p t m", t=PACK),
+        )
+        gather_rows(w2_plane, 0)
 
         h_banks = {}
 
@@ -143,7 +145,7 @@ def tile_picked_zres_gelu_po_kernel(
                 lhsT=w1_codes[a][:, t * P : (t + 1) * P].bitcast(FP8X4),
                 lhsT_scale=w1_plane[a][:, t * P : (t + 1) * P],
                 rhs=x_picked[a, n0].bitcast(FP8X4),
-                rhs_scale=x_picked_plane[4 * a : P, n0 : n0 + BLOCK],
+                rhs_scale=x_planes[a][4 * a : P, n0 : n0 + BLOCK],
                 start=(opens and t == 0),
                 stop=(closes and t == PACK - 1),
             )
@@ -156,10 +158,10 @@ def tile_picked_zres_gelu_po_kernel(
         for n0 in range(0, OPEN_BLOCKS * BLOCK, BLOCK):
             open_block(n0, 0)
 
-        nc.scalar.copy(*w1_views(1, 0, SCALAR_SHARE))
-        nc.vector.tensor_copy(*w1_views(1, SCALAR_SHARE, P))
+        nc.scalar.copy(*w1_views(1, 0, SCALAR_SHARES[1]))
+        nc.vector.tensor_copy(*w1_views(1, SCALAR_SHARES[1], P))
         nc.vector.quantize_mx(w1_codes[1][:].bitcast(FP8X4), w1_plane[1][:], w1_bf[1][:])
-        last_picked = shared.tile([P, sum(GATHERS)], U32, name="last_picked", align_bytes=64, offset=held + 2048)
+        last_picked = keep.tile([P, sum(GATHERS)], U32, name="last_picked", align_bytes=64)
         for i, width in enumerate(GATHERS):
             n0 = sum(GATHERS[:i])
             gather_x(1, n0, last_picked[:, n0 : n0 + width])
@@ -186,14 +188,14 @@ def tile_picked_zres_gelu_po_kernel(
         def span_of(spans, n):
             return max(span for span in spans if span[0] <= n)
 
-        ring = held + 8192
+        ring = held + 12288
         g_bf = tiles(shared, "g_bf", BF16, PACK, G_SPANS, {0: ring, 128: ring + 1024, 384: ring + 3072, 640: ring + 5120, 896: 2048 + ring + 7168})
-        late_picked = shared.tile([P, S - sum(GATHERS)], U32, name="late_picked", align_bytes=64, offset=ring + 1024)
         g_codes = tiles(keep, "g_codes", U32, 1, G_SPANS)
         g_plane = tiles(keep, "g_plane", U8, 1, G_SPANS)
         h_kept = tiles(keep, "h_kept", F32, PACK, PIECES)
         result = tiles(keep, "result", F32, PACK, PIECES)
-        result_bf = tiles(shared, "result_bf", BF16, PACK, ROUNDED, {0: 4096, 128: 4096, 384: ring + 7168 + 1024, 640: 8192, 896: 10240})
+        result[640] = shared.tile([P, BLOCK * PACK], F32, name="result_late", align_bytes=64, offset=ring + 9728)
+        result_bf = tiles(shared, "result_bf", BF16, PACK, ROUNDED, {0: ring + 2048, 128: ring + 2560, 384: ring + 7680, 640: ring + 14336, 896: ring + 16384})
 
         def quarters_of(tile):
             return tile[:].rearrange("p (t n) -> p t n", t=PACK)
@@ -284,29 +286,28 @@ def tile_picked_zres_gelu_po_kernel(
         project(1)
         quantize_g(0)
         keep_h(0)
-        branch(0)
         project(2)
-        keep_h(1)
         quantize_g(128)
-        gather_x(1, sum(GATHERS), late_picked[:])
+        branch(0)
+        keep_h(1)
         round_result(0)
         keep_h(2)
         branch(128)
         project(3)
         project(4)
         keep_h(3)
-        quantize_g(384)
         quantize_result(0)
+        quantize_g(384)
         round_result(128)
         keep_h(4)
         branch(384)
         project(5)
         project(6)
-        keep_h(5)
         project(7)
+        keep_h(5)
         quantize_g(640)
-        quantize_result(128)
         quantize_g(896)
+        quantize_result(128)
         round_result(384)
         for b in range(5, 8):
             if b > 5:

@@ -23,12 +23,13 @@ PACK = 4
 PASSES = K // (P * PACK)
 QUADS = 4
 BLOCK = 128
-GATHERS = (128, 128, 256, 256, 256)
+GATHERS = (128, 128, 256, 512)
 SCALAR_SHARES = (100, 76)
 FIRST_PIECE = 3 * T // 8
 G_SPANS = ((0, 128), (128, 256), (384, 256), (640, 256), (896, 128))
 PIECES = ((0, 128), (128, 256), (384, 256), (640, 128), (768, 128), (896, 128))
 ROUNDED = G_SPANS
+STORED_IN_HALVES = (640, 768)
 H_ON_VECTOR = (0, 4)
 ROUND_ON_GPSIMD = (0, 128, 384)
 H_BANKS = 4
@@ -87,8 +88,7 @@ def tile_picked_zres_gelu_po_kernel(
 
         load_x(0, 0, FIRST_PIECE)
         nc.sync.dma_start(offsets[:], offs)
-        for a in range(PASSES):
-            nc.sync.dma_start(x_rows[4 * a : P : 8, :].bitcast(I32), x_scales[a].bitcast(I32))
+        nc.sync.dma_start(x_rows[0:P:4, :].bitcast(I32), x_scales.bitcast(I32).rearrange("a q n -> q a n"))
         nc.sync.dma_start(w2_rows[0:P:8, :].bitcast(I32), w2_scales[0].bitcast(I32))
         load_x(0, FIRST_PIECE, T)
         nc.sync.dma_start(turn_row[0:1, :], turn.rearrange("m o -> o m"))
@@ -244,6 +244,7 @@ def tile_picked_zres_gelu_po_kernel(
                         start=True,
                         stop=True,
                     )
+                step = 2 if n0 in STORED_IN_HALVES else per_bank
                 for t in range(t0, t0 + per_bank):
                     nc.vector.scalar_tensor_tensor(
                         quarters_of(result[n0])[:, t, :],
@@ -253,8 +254,9 @@ def tile_picked_zres_gelu_po_kernel(
                         MULT,
                         ADD,
                     )
-                quarters = slice(t0, t0 + per_bank)
-                nc.sync.dma_start(out_rows[:, quarters, n0 : n0 + w], quarters_of(result[n0])[:, quarters, :])
+                    if (t + 1) % step == 0:
+                        quarters = slice(t + 1 - step, t + 1)
+                        nc.sync.dma_start(out_rows[:, quarters, n0 : n0 + w], quarters_of(result[n0])[:, quarters, :])
 
         def round_result(n0):
             w = span_of(PIECES, n0)[1]

@@ -22,20 +22,41 @@ P = 128
 PACK = 4
 PASSES = K // (P * PACK)
 QUADS = 4
-BLOCK = 128
-GATHERS = (128, 128, 256, 512)
-SCALAR_SHARES = (100, 76)
+BANK = 512
+BLOCK = BANK // PACK
+
 FIRST_PIECE = 3 * T // 8
-G_SPANS = ((0, 128), (128, 256), (384, 256), (640, 256), (896, 128))
-PIECES = ((0, 128), (128, 256), (384, 256), (640, 128), (768, 128), (896, 128))
-ROUNDED = G_SPANS
-STORED_IN_HALVES = (640, 768)
-H_ON_VECTOR = (0, 4)
-ROUND_ON_GPSIMD = (0, 128, 384)
+SCALAR_SHARES = (100, 76)
+OPEN_BLOCKS = 3
+GATHERS = (128, 128, 256, 512)
 H_BANKS = 4
 Y_BANKS = 3
-OPEN_BLOCKS = 3
-CODE_STORES = {128: 0, 640: 384, 896: 896}
+SPANS = ((0, 128), (128, 256), (384, 256), (640, 256), (896, 128))
+PIECES = ((0, 128), (128, 256), (384, 256), (640, 128), (768, 128), (896, 128))
+H_ON_VECTOR = (0, 4)
+ROUND_ON_GPSIMD = (0, 128, 384)
+STORED_IN_HALVES = (640,)
+CODE_STORES = {128: 0, 384: 384, 896: 640}
+
+KIB = 1024
+X_ROWS_AT = 0
+X_TABLE1_AT = 4 * KIB
+HELD = X_TABLE1_AT + 4 * T
+PICKED_ROWS_AT = HELD - 128
+W2_RAW_AT = HELD + 64
+W1_BF_AT = (HELD + 6 * KIB, HELD + 2 * KIB)
+W2_PLANE_AT = W1_BF_AT[0]
+RING = HELD + 12 * KIB
+G_BF_AT = {0: RING, 128: RING + KIB, 384: RING + 3 * KIB, 640: RING + 5 * KIB, 896: RING + 9 * KIB}
+RESULT_BF_AT = {
+    0: RING + 2 * KIB,
+    128: RING + 5 * KIB // 2,
+    384: RING + 15 * KIB // 2,
+    640: RING + 14 * KIB,
+    896: RING + 16 * KIB,
+}
+HELD_PIECE = 640
+HELD_PIECE_AT = RING + 19 * KIB // 2
 
 
 def tile_picked_zres_gelu_po_kernel(
@@ -48,7 +69,7 @@ def tile_picked_zres_gelu_po_kernel(
         psum = ctx.enter_context(tc.psum_pool(name="psum", bufs=4))
 
         offsets = keep.tile([P, S // 16], U16, name="offsets")
-        x_rows = shared.tile([P, T], U8, name="x_rows", align_bytes=64, offset=0)
+        x_rows = shared.tile([P, T], U8, name="x_rows", align_bytes=64, offset=X_ROWS_AT)
         w2_rows = keep.tile([P, H], U8, name="w2_rows", align_bytes=64)
         warm = keep.tile([P, 8], F32, name="warm")
         warm_out = keep.tile([P, 8], F32, name="warm_out")
@@ -62,25 +83,24 @@ def tile_picked_zres_gelu_po_kernel(
         nc.vector.memset(identity[:], 0.0)
         make_identity(nc, identity[:], nomemset=True)
 
-        held = 4096 + 4 * T
-        picked_rows = shared.tile([P, S], U8, name="picked_rows", align_bytes=64, offset=held - 128)
+        picked_rows = shared.tile([P, S], U8, name="picked_rows", align_bytes=64, offset=PICKED_ROWS_AT)
         w1_raw = [keep.tile([P, PACK, H], F32, name="w1_raw%d" % a) for a in range(PASSES)]
         x_table = [
             keep.tile([P, T], U32, name="x_table0", align_bytes=64),
-            shared.tile([P, T], U32, name="x_table1", align_bytes=64, offset=4096),
+            shared.tile([P, T], U32, name="x_table1", align_bytes=64, offset=X_TABLE1_AT),
         ]
-        w2_raw = shared.tile([P, 2 * H], U8, name="w2_raw", align_bytes=64, offset=held + 64)
+        w2_raw = shared.tile([P, 2 * H], U8, name="w2_raw", align_bytes=64, offset=W2_RAW_AT)
         x_planes = [keep.tile([P, S], U8, name="x_plane%d" % a, align_bytes=64) for a in range(PASSES)]
 
         def load_w1(a):
-            rows = w1[a * 512 : (a + 1) * 512, :].rearrange("(p j) c -> p j c", j=PACK)
+            rows = w1[a * P * PACK : (a + 1) * P * PACK, :].rearrange("(p j) c -> p j c", j=PACK)
             nc.sync.dma_start(w1_raw[a][:], rows)
 
         def load_x(a, n0, n1):
             words = x_words[a].rearrange("p n t -> p (n t)").bitcast(I32)
             nc.sync.dma_start(x_table[a][:, n0:n1].bitcast(I32), words[:, n0:n1])
 
-        def gather_rows(plane, first):
+        def place_rows(plane, first):
             for r in range(1, 4):
                 nc.sync.dma_start(
                     plane[first + r : P : 32, :].bitcast(I32), plane[first + 8 * r : P : 32, :].bitcast(I32)
@@ -97,28 +117,32 @@ def tile_picked_zres_gelu_po_kernel(
         nc.vector.tensor_copy(picked_rows[:], x_rows[:].indirect(offsets[:]))
         for a in range(PASSES):
             nc.vector.tensor_copy(x_planes[a][:].bitcast(I32), picked_rows[:].bitcast(I32))
-        gather_rows(x_planes[0], 0)
+        place_rows(x_planes[0], 0)
         load_x(1, 0, T)
         nc.sync.dma_start(w2_raw[:].bitcast(I32), w2_words[0].bitcast(I32))
-        gather_rows(x_planes[1], 4)
+        place_rows(x_planes[1], 4)
         factor = psum.tile([P, PACK, P], F32, name="factor", bufs=1)
         for t in range(PACK):
             nc.tensor.transpose(factor[:, t, :], turn_row[:, t:H:PACK], identity[:])
 
         w1_bf = [
-            shared.tile([P, H * PACK], BF16, name="w1_bf0", align_bytes=64, offset=held + 6144),
-            shared.tile([P, H * PACK], BF16, name="w1_bf1", align_bytes=64, offset=held + 2048),
+            shared.tile([P, H * PACK], BF16, name="w1_bf%d" % a, align_bytes=64, offset=W1_BF_AT[a])
+            for a in range(PASSES)
         ]
         w1_codes = [keep.tile([P, H], U32, name="w1_codes%d" % a, align_bytes=64) for a in range(PASSES)]
         w1_plane = [keep.tile([P, H], U8, name="w1_plane%d" % a, align_bytes=64) for a in range(PASSES)]
-        w2_plane = shared.tile([P, H], U8, name="w2_plane", align_bytes=64, offset=held + 6144)
-        x_picked = {}
+        w2_plane = shared.tile([P, H], U8, name="w2_plane", align_bytes=64, offset=W2_PLANE_AT)
         w2_codes = keep.tile([P, 2 * H], U8, name="w2_codes", align_bytes=64)
 
-        def w1_views(a, m0, m1):
+        def quantize_w1(a):
             dst = w1_bf[a][:].rearrange("p (t m j) -> p m j t", t=PACK, j=PACK)
             src = w1_raw[a][:].rearrange("p j (m t) -> p m j t", t=PACK)
-            return dst[:, m0:m1], src[:, m0:m1]
+            share = SCALAR_SHARES[a]
+            nc.scalar.copy(dst[:, :share], src[:, :share])
+            nc.vector.tensor_copy(dst[:, share:], src[:, share:])
+            nc.vector.quantize_mx(w1_codes[a][:].bitcast(FP8X4), w1_plane[a][:], w1_bf[a][:])
+
+        x_picked = {}
 
         def gather_x(a, n0, picked):
             n1 = n0 + picked.shape[1]
@@ -126,42 +150,38 @@ def tile_picked_zres_gelu_po_kernel(
             for n in range(n0, n1, BLOCK):
                 x_picked[a, n] = picked[:, n - n0 : n - n0 + BLOCK]
 
-        first_picked = shared.tile([P, S], U32, name="first_picked", align_bytes=64, offset=0)
+        first_picked = shared.tile([P, S], U32, name="first_picked", align_bytes=64, offset=X_ROWS_AT)
         gather_x(0, 0, first_picked[:])
-        nc.scalar.copy(*w1_views(0, 0, SCALAR_SHARES[0]))
-        nc.vector.tensor_copy(*w1_views(0, SCALAR_SHARES[0], P))
-        nc.vector.quantize_mx(w1_codes[0][:].bitcast(FP8X4), w1_plane[0][:], w1_bf[0][:])
+        quantize_w1(0)
         nc.vector.tensor_copy(
             w2_plane[:].rearrange("p (t m) -> p t m", t=PACK),
             w2_rows[:].rearrange("p (m t) -> p t m", t=PACK),
         )
-        gather_rows(w2_plane, 0)
+        place_rows(w2_plane, 0)
 
         h_banks = {}
 
-        def product_pass(n0, a, t, opens, closes):
-            nc.tensor.matmul_mx(
-                h_banks[n0][:, t, :],
-                lhsT=w1_codes[a][:, t * P : (t + 1) * P].bitcast(FP8X4),
-                lhsT_scale=w1_plane[a][:, t * P : (t + 1) * P],
-                rhs=x_picked[a, n0].bitcast(FP8X4),
-                rhs_scale=x_planes[a][4 * a : P, n0 : n0 + BLOCK],
-                start=(opens and t == 0),
-                stop=(closes and t == PACK - 1),
-            )
+        def product_pass(n0, a, opens):
+            for t in range(PACK):
+                nc.tensor.matmul_mx(
+                    h_banks[n0][:, t, :],
+                    lhsT=w1_codes[a][:, t * P : (t + 1) * P].bitcast(FP8X4),
+                    lhsT_scale=w1_plane[a][:, t * P : (t + 1) * P],
+                    rhs=x_picked[a, n0].bitcast(FP8X4),
+                    rhs_scale=x_planes[a][4 * a : P, n0 : n0 + BLOCK],
+                    start=(opens and t == 0),
+                    stop=(not opens and t == PACK - 1),
+                )
 
         def open_block(n0, a):
             h_banks[n0] = psum.tile([P, PACK, BLOCK], F32, name="h_bank", bufs=H_BANKS)
-            for t in range(PACK):
-                product_pass(n0, a, t, True, False)
+            product_pass(n0, a, True)
 
         for n0 in range(0, OPEN_BLOCKS * BLOCK, BLOCK):
             open_block(n0, 0)
 
-        nc.scalar.copy(*w1_views(1, 0, SCALAR_SHARES[1]))
-        nc.vector.tensor_copy(*w1_views(1, SCALAR_SHARES[1], P))
-        nc.vector.quantize_mx(w1_codes[1][:].bitcast(FP8X4), w1_plane[1][:], w1_bf[1][:])
-        last_picked = keep.tile([P, sum(GATHERS)], U32, name="last_picked", align_bytes=64)
+        quantize_w1(1)
+        last_picked = keep.tile([P, S], U32, name="last_picked", align_bytes=64)
         for i, width in enumerate(GATHERS):
             n0 = sum(GATHERS[:i])
             gather_x(1, n0, last_picked[:, n0 : n0 + width])
@@ -176,38 +196,39 @@ def tile_picked_zres_gelu_po_kernel(
         out_rows = out_0.rearrange("(p t) n -> p t n", t=PACK)
         out_words = out_1[0].rearrange("p n t -> p (n t)").bitcast(I32)
 
-        def tiles(pool, name, dtype, per_token, spans, at=None):
+        def kept_tiles(name, dtype, per_token, spans):
             return {
-                n0: pool.tile(
-                    [P, w * per_token], dtype, name="%s%d" % (name, n0), align_bytes=64,
-                    **({} if at is None else {"offset": at[n0]})
-                )
-                for n0, w in spans
+                n0: keep.tile([P, w * per_token], dtype, name="%s%d" % (name, n0), align_bytes=64) for n0, w in spans
+            }
+
+        def staged_tiles(name, at):
+            return {
+                n0: shared.tile([P, w * PACK], BF16, name="%s%d" % (name, n0), align_bytes=64, offset=at[n0])
+                for n0, w in SPANS
             }
 
         def span_of(spans, n):
             return max(span for span in spans if span[0] <= n)
 
-        ring = held + 12288
-        g_bf = tiles(shared, "g_bf", BF16, PACK, G_SPANS, {0: ring, 128: ring + 1024, 384: ring + 3072, 640: ring + 5120, 896: 2048 + ring + 7168})
-        g_codes = tiles(keep, "g_codes", U32, 1, G_SPANS)
-        g_plane = tiles(keep, "g_plane", U8, 1, G_SPANS)
-        h_kept = tiles(keep, "h_kept", F32, PACK, PIECES)
-        result = tiles(keep, "result", F32, PACK, PIECES)
-        result[640] = shared.tile([P, BLOCK * PACK], F32, name="result_late", align_bytes=64, offset=ring + 9728)
-        result_bf = tiles(shared, "result_bf", BF16, PACK, ROUNDED, {0: ring + 2048, 128: ring + 2560, 384: ring + 7680, 640: ring + 14336, 896: ring + 16384})
-
         def quarters_of(tile):
             return tile[:].rearrange("p (t n) -> p t n", t=PACK)
 
+        g_bf = staged_tiles("g_bf", G_BF_AT)
+        g_codes = kept_tiles("g_codes", U32, 1, SPANS)
+        g_plane = kept_tiles("g_plane", U8, 1, SPANS)
+        h_kept = kept_tiles("h_kept", F32, PACK, PIECES)
+        result = kept_tiles("result", F32, PACK, [piece for piece in PIECES if piece[0] != HELD_PIECE])
+        result[HELD_PIECE] = shared.tile([P, BANK], F32, name="result_held", align_bytes=64, offset=HELD_PIECE_AT)
+        result_bf = staged_tiles("result_bf", RESULT_BF_AT)
+
         def project(b):
             n0 = b * BLOCK
-            closing = 1 if n0 in h_banks else 0
-            if n0 not in h_banks:
+            if n0 in h_banks:
+                product_pass(n0, 1, False)
+            else:
                 open_block(n0, 1)
-            for t in range(PACK):
-                product_pass(n0, closing, t, False, True)
-            first = span_of(G_SPANS, n0)[0]
+                product_pass(n0, 0, False)
+            first = span_of(SPANS, n0)[0]
             local = n0 - first
             nc.scalar.activation(
                 g_bf[first][:, local * PACK : (local + BLOCK) * PACK].rearrange("p (n t) -> p n t", t=PACK),
@@ -229,11 +250,12 @@ def tile_picked_zres_gelu_po_kernel(
 
         def branch(n0):
             w = span_of(PIECES, n0)[1]
-            first = span_of(G_SPANS, n0)[0]
+            first = span_of(SPANS, n0)[0]
             cols = slice(n0 - first, n0 - first + w)
-            per_bank = 512 // w
+            per_bank = BANK // w
+            per_store = PACK // 2 if n0 in STORED_IN_HALVES else per_bank
             for t0 in range(0, PACK, per_bank):
-                bank = psum.tile([P, 512], F32, name="y_bank", bufs=Y_BANKS)
+                bank = psum.tile([P, BANK], F32, name="y_bank", bufs=Y_BANKS)
                 for t in range(t0, t0 + per_bank):
                     nc.tensor.matmul_mx(
                         bank[:, (t - t0) * w : (t - t0 + 1) * w],
@@ -244,7 +266,6 @@ def tile_picked_zres_gelu_po_kernel(
                         start=True,
                         stop=True,
                     )
-                step = 2 if n0 in STORED_IN_HALVES else per_bank
                 for t in range(t0, t0 + per_bank):
                     nc.vector.scalar_tensor_tensor(
                         quarters_of(result[n0])[:, t, :],
@@ -254,17 +275,17 @@ def tile_picked_zres_gelu_po_kernel(
                         MULT,
                         ADD,
                     )
-                    if (t + 1) % step == 0:
-                        quarters = slice(t + 1 - step, t + 1)
+                    if (t + 1) % per_store == 0:
+                        quarters = slice(t + 1 - per_store, t + 1)
                         nc.sync.dma_start(out_rows[:, quarters, n0 : n0 + w], quarters_of(result[n0])[:, quarters, :])
 
         def round_result(n0):
             w = span_of(PIECES, n0)[1]
-            first = span_of(ROUNDED, n0)[0]
-            out = result_bf[first][:, (n0 - first) * PACK : (n0 - first + w) * PACK]
+            first = span_of(SPANS, n0)[0]
+            rounded = result_bf[first][:, (n0 - first) * PACK : (n0 - first + w) * PACK]
             if n0 in ROUND_ON_GPSIMD:
                 nc.gpsimd.tensor_scalar(
-                    out.rearrange("p (n t) -> p n t", t=PACK),
+                    rounded.rearrange("p (n t) -> p n t", t=PACK),
                     result[n0][:].rearrange("p (t n) -> p n t", t=PACK),
                     1.0,
                     0.0,
@@ -273,53 +294,55 @@ def tile_picked_zres_gelu_po_kernel(
                 )
             else:
                 nc.scalar.copy(
-                    out.rearrange("p (n i t) -> p n t i", i=4, t=PACK),
+                    rounded.rearrange("p (n i t) -> p n t i", i=4, t=PACK),
                     result[n0][:].rearrange("p (t n i) -> p n t i", i=4, t=PACK),
                 )
 
         def quantize_result(n0):
-            cols = slice(n0, n0 + span_of(ROUNDED, n0)[1])
+            cols = slice(n0, n0 + span_of(SPANS, n0)[1])
             nc.vector.quantize_mx(out_codes[:, cols].bitcast(FP8X4), out_plane[:, cols], result_bf[n0][:])
             if n0 in CODE_STORES:
                 cols = slice(CODE_STORES[n0], cols.stop)
                 nc.sync.dma_start(out_words[:, cols], out_codes[:, cols].bitcast(I32))
 
+        span = [n0 for n0, w in SPANS]
         project(0)
         project(1)
-        quantize_g(0)
+        quantize_g(span[0])
         keep_h(0)
         project(2)
-        quantize_g(128)
-        branch(0)
+        quantize_g(span[1])
+        branch(span[0])
         keep_h(1)
-        round_result(0)
+        round_result(span[0])
         keep_h(2)
-        branch(128)
+        branch(span[1])
+
         project(3)
         project(4)
         keep_h(3)
-        quantize_result(0)
-        quantize_g(384)
-        round_result(128)
+        quantize_result(span[0])
+        quantize_g(span[2])
+        round_result(span[1])
         keep_h(4)
-        branch(384)
-        project(5)
-        project(6)
-        project(7)
-        keep_h(5)
-        quantize_g(640)
-        quantize_g(896)
-        quantize_result(128)
-        round_result(384)
-        for b in range(5, 8):
-            if b > 5:
-                keep_h(b)
+        branch(span[2])
+
+        last_blocks = range(span[3] // BLOCK, S // BLOCK)
+        for b in last_blocks:
+            project(b)
+        keep_h(last_blocks[0])
+        quantize_g(span[3])
+        quantize_g(span[4])
+        quantize_result(span[1])
+        round_result(span[2])
+        branch(last_blocks[0] * BLOCK)
+        for b in last_blocks[1:]:
+            keep_h(b)
             branch(b * BLOCK)
-        for b in range(5, 8):
+        for b in last_blocks:
             round_result(b * BLOCK)
-        quantize_result(384)
-        quantize_result(640)
-        quantize_result(896)
+        for n0 in span[2:]:
+            quantize_result(n0)
 
         for q in range(QUADS):
             queue = nc.sync if q % 2 == 0 else nc.scalar

@@ -36,7 +36,7 @@ PIECES = ((0, 128), (128, 256), (384, 256), (640, 128), (768, 128), (896, 128))
 H_ON_VECTOR = (0, 4)
 ROUND_ON_GPSIMD = (0, 128, 384)
 STORED_IN_HALVES = (640,)
-CODE_STORES = {128: 0, 384: 384, 896: 640}
+CODE_STORES = {128: 0, 896: 384}
 
 KIB = 1024
 X_ROWS_AT = 0

@@ -31,11 +31,12 @@ OPEN_BLOCKS = 3
 GATHERS = (128, 128, 256, 512)
 H_BANKS = 4
 Y_BANKS = 3
-SPANS = ((0, 128), (128, 256), (384, 256), (640, 256), (896, 128))
+G_SPANS = ((0, 128), (128, 256), (384, 256), (640, 256), (896, 128))
+OUT_SPANS = G_SPANS
 PIECES = ((0, 128), (128, 256), (384, 256), (640, 128), (768, 128), (896, 128))
+RESULTS = ((0, 128), (128, 256), (384, 256), (640, 128), (768, 256))
 H_ON_VECTOR = (0, 4)
-ROUND_ON_GPSIMD = (0, 128, 384)
-STORED_IN_HALVES = (640,)
+STORED = {0: 4, 128: 2, 384: 2, 640: 4, 896: 2}
 CODE_STORES = {128: 0, 896: 384}
 
 KIB = 1024
@@ -201,10 +202,10 @@ def tile_picked_zres_gelu_po_kernel(
                 n0: keep.tile([P, w * per_token], dtype, name="%s%d" % (name, n0), align_bytes=64) for n0, w in spans
             }
 
-        def staged_tiles(name, at):
+        def staged_tiles(name, at, spans):
             return {
                 n0: shared.tile([P, w * PACK], BF16, name="%s%d" % (name, n0), align_bytes=64, offset=at[n0])
-                for n0, w in SPANS
+                for n0, w in spans
             }
 
         def span_of(spans, n):
@@ -213,13 +214,13 @@ def tile_picked_zres_gelu_po_kernel(
         def quarters_of(tile):
             return tile[:].rearrange("p (t n) -> p t n", t=PACK)
 
-        g_bf = staged_tiles("g_bf", G_BF_AT)
-        g_codes = kept_tiles("g_codes", U32, 1, SPANS)
-        g_plane = kept_tiles("g_plane", U8, 1, SPANS)
+        g_bf = staged_tiles("g_bf", G_BF_AT, G_SPANS)
+        g_codes = kept_tiles("g_codes", U32, 1, G_SPANS)
+        g_plane = kept_tiles("g_plane", U8, 1, G_SPANS)
         h_kept = kept_tiles("h_kept", F32, PACK, PIECES)
-        result = kept_tiles("result", F32, PACK, [piece for piece in PIECES if piece[0] != HELD_PIECE])
+        result = kept_tiles("result", F32, PACK, [span for span in RESULTS if span[0] != HELD_PIECE])
         result[HELD_PIECE] = shared.tile([P, BANK], F32, name="result_held", align_bytes=64, offset=HELD_PIECE_AT)
-        result_bf = staged_tiles("result_bf", RESULT_BF_AT)
+        result_bf = staged_tiles("result_bf", RESULT_BF_AT, OUT_SPANS)
 
         def project(b):
             n0 = b * BLOCK
@@ -228,7 +229,7 @@ def tile_picked_zres_gelu_po_kernel(
             else:
                 open_block(n0, 1)
                 product_pass(n0, 0, False)
-            first = span_of(SPANS, n0)[0]
+            first = span_of(G_SPANS, n0)[0]
             local = n0 - first
             nc.scalar.activation(
                 g_bf[first][:, local * PACK : (local + BLOCK) * PACK].rearrange("p (n t) -> p n t", t=PACK),
@@ -248,100 +249,101 @@ def tile_picked_zres_gelu_po_kernel(
         def quantize_g(n0):
             nc.vector.quantize_mx(g_codes[n0][:].bitcast(FP8X4), g_plane[n0][:], g_bf[n0][:])
 
-        def branch(n0):
+        def branch(n0, t0, t1):
             w = span_of(PIECES, n0)[1]
-            first = span_of(SPANS, n0)[0]
+            first = span_of(G_SPANS, n0)[0]
             cols = slice(n0 - first, n0 - first + w)
-            per_bank = BANK // w
-            per_store = PACK // 2 if n0 in STORED_IN_HALVES else per_bank
-            for t0 in range(0, PACK, per_bank):
-                bank = psum.tile([P, BANK], F32, name="y_bank", bufs=Y_BANKS)
-                for t in range(t0, t0 + per_bank):
-                    nc.tensor.matmul_mx(
-                        bank[:, (t - t0) * w : (t - t0 + 1) * w],
-                        lhsT=w2_codes[:, t * 2 * P : (t + 1) * 2 * P].bitcast(FP4X4),
-                        lhsT_scale=w2_plane[:, t * P : (t + 1) * P],
-                        rhs=g_codes[first][:, cols].bitcast(FP8X4),
-                        rhs_scale=g_plane[first][:, cols],
-                        start=True,
-                        stop=True,
-                    )
-                for t in range(t0, t0 + per_bank):
-                    nc.vector.scalar_tensor_tensor(
-                        quarters_of(result[n0])[:, t, :],
-                        bank[:, (t - t0) * w : (t - t0 + 1) * w],
-                        factor[:, t, 0:1],
-                        quarters_of(h_kept[n0])[:, t, :],
-                        MULT,
-                        ADD,
-                    )
-                    if (t + 1) % per_store == 0:
-                        quarters = slice(t + 1 - per_store, t + 1)
-                        nc.sync.dma_start(out_rows[:, quarters, n0 : n0 + w], quarters_of(result[n0])[:, quarters, :])
-
-        def round_result(n0):
-            w = span_of(PIECES, n0)[1]
-            first = span_of(SPANS, n0)[0]
-            rounded = result_bf[first][:, (n0 - first) * PACK : (n0 - first + w) * PACK]
-            if n0 in ROUND_ON_GPSIMD:
-                nc.gpsimd.tensor_scalar(
-                    rounded.rearrange("p (n t) -> p n t", t=PACK),
-                    result[n0][:].rearrange("p (t n) -> p n t", t=PACK),
-                    1.0,
-                    0.0,
+            r0, rw = span_of(RESULTS, n0)
+            bank = psum.tile([P, BANK], F32, name="y_bank", bufs=Y_BANKS)
+            for t in range(t0, t1):
+                nc.tensor.matmul_mx(
+                    bank[:, (t - t0) * w : (t - t0 + 1) * w],
+                    lhsT=w2_codes[:, t * 2 * P : (t + 1) * 2 * P].bitcast(FP4X4),
+                    lhsT_scale=w2_plane[:, t * P : (t + 1) * P],
+                    rhs=g_codes[first][:, cols].bitcast(FP8X4),
+                    rhs_scale=g_plane[first][:, cols],
+                    start=True,
+                    stop=True,
+                )
+            for t in range(t0, t1):
+                nc.vector.scalar_tensor_tensor(
+                    quarters_of(result[r0])[:, t, n0 - r0 : n0 - r0 + w],
+                    bank[:, (t - t0) * w : (t - t0 + 1) * w],
+                    factor[:, t, 0:1],
+                    quarters_of(h_kept[n0])[:, t, :],
                     MULT,
                     ADD,
                 )
-            else:
-                nc.scalar.copy(
-                    rounded.rearrange("p (n i t) -> p n t i", i=4, t=PACK),
-                    result[n0][:].rearrange("p (t n i) -> p n t i", i=4, t=PACK),
-                )
+                if n0 in STORED and (t + 1) % STORED[n0] == 0:
+                    quarters = slice(t + 1 - STORED[n0], t + 1)
+                    nc.sync.dma_start(out_rows[:, quarters, r0 : r0 + rw], quarters_of(result[r0])[:, quarters, :])
+
+        def rounding_views(n0, w):
+            piece = span_of(RESULTS, n0)[0]
+            first = span_of(OUT_SPANS, n0)[0]
+            rounded = result_bf[first][:, (n0 - first) * PACK : (n0 - first + w) * PACK]
+            return rounded, quarters_of(result[piece])[:, :, n0 - piece : n0 - piece + w]
+
+        def round_on_gpsimd(n0, w):
+            rounded, exact = rounding_views(n0, w)
+            nc.gpsimd.tensor_scalar(
+                rounded.rearrange("p (n t) -> p n t", t=PACK), exact.rearrange("p t n -> p n t"), 1.0, 0.0, MULT, ADD
+            )
+
+        def round_by(copy, n0, w):
+            rounded, exact = rounding_views(n0, w)
+            copy(
+                rounded.rearrange("p (n i t) -> p n t i", i=4, t=PACK), exact.rearrange("p t (n i) -> p n t i", i=4)
+            )
 
         def quantize_result(n0):
-            cols = slice(n0, n0 + span_of(SPANS, n0)[1])
+            cols = slice(n0, n0 + span_of(OUT_SPANS, n0)[1])
             nc.vector.quantize_mx(out_codes[:, cols].bitcast(FP8X4), out_plane[:, cols], result_bf[n0][:])
             if n0 in CODE_STORES:
                 cols = slice(CODE_STORES[n0], cols.stop)
                 nc.sync.dma_start(out_words[:, cols], out_codes[:, cols].bitcast(I32))
 
-        span = [n0 for n0, w in SPANS]
+        half = PACK // 2
+
+        def wide_branch(n0):
+            branch(n0, 0, half)
+            branch(n0, half, PACK)
+
         project(0)
         project(1)
-        quantize_g(span[0])
+        quantize_g(0)
         keep_h(0)
         project(2)
-        quantize_g(span[1])
-        branch(span[0])
+        quantize_g(128)
+        branch(0, 0, PACK)
         keep_h(1)
-        round_result(span[0])
+        round_on_gpsimd(0, BLOCK)
         keep_h(2)
-        branch(span[1])
+        wide_branch(128)
 
         project(3)
         project(4)
         keep_h(3)
-        quantize_result(span[0])
-        quantize_g(span[2])
-        round_result(span[1])
+        quantize_result(0)
+        quantize_g(384)
+        round_on_gpsimd(128, 2 * BLOCK)
         keep_h(4)
-        branch(span[2])
+        wide_branch(384)
 
-        last_blocks = range(span[3] // BLOCK, S // BLOCK)
-        for b in last_blocks:
+        for b in range(5, 8):
             project(b)
-        keep_h(last_blocks[0])
-        quantize_g(span[3])
-        quantize_g(span[4])
-        quantize_result(span[1])
-        round_result(span[2])
-        branch(last_blocks[0] * BLOCK)
-        for b in last_blocks[1:]:
+        keep_h(5)
+        quantize_g(640)
+        quantize_g(896)
+        quantize_result(128)
+        round_on_gpsimd(384, 2 * BLOCK)
+        branch(640, 0, PACK)
+        for b in range(6, 8):
             keep_h(b)
-            branch(b * BLOCK)
-        for b in last_blocks:
-            round_result(b * BLOCK)
-        for n0 in span[2:]:
+            branch(b * BLOCK, 0, PACK)
+        for b in range(5, 8):
+            round_by(nc.scalar.copy, b * BLOCK, BLOCK)
+        for n0 in (384, 640, 896):
             quantize_result(n0)
 
         for q in range(QUADS):

@@ -34,10 +34,10 @@ Y_BANKS = 3
 G_SPANS = ((0, 128), (128, 256), (384, 256), (640, 256), (896, 128))
 OUT_SPANS = G_SPANS
 PIECES = ((0, 128), (128, 256), (384, 256), (640, 128), (768, 128), (896, 128))
-RESULTS = ((0, 128), (128, 256), (384, 256), (640, 128), (768, 256))
+RESULTS = ((0, 384), (384, 256), (640, 128), (768, 256))
 H_ON_VECTOR = (0, 4)
-STORED = {0: 4, 128: 2, 384: 2, 640: 4, 896: 2}
-CODE_STORES = {128: 0, 896: 384}
+STORED = {128: 2, 384: 2, 640: 4, 896: 2}
+CODE_STORES = {128: 0, 640: 384, 896: 896}
 
 KIB = 1024
 X_ROWS_AT = 0

@@ -110,9 +110,9 @@ def tile_picked_zres_gelu_po_kernel(
         load_x(0, 0, FIRST_PIECE)
         nc.sync.dma_start(offsets[:], offs)
         nc.sync.dma_start(x_rows[0:P:4, :].bitcast(I32), x_scales.bitcast(I32).rearrange("a q n -> q a n"))
-        nc.sync.dma_start(w2_rows[0:P:8, :].bitcast(I32), w2_scales[0].bitcast(I32))
+        nc.scalar.dma_start(w2_rows[0:P:8, :].bitcast(I32), w2_scales[0].bitcast(I32))
         load_x(0, FIRST_PIECE, T)
-        nc.sync.dma_start(turn_row[0:1, :], turn.rearrange("m o -> o m"))
+        nc.scalar.dma_start(turn_row[0:1, :], turn.rearrange("m o -> o m"))
         load_w1(0)
         load_w1(1)
         nc.vector.tensor_copy(picked_rows[:], x_rows[:].indirect(offsets[:]))

@@ -21,7 +21,6 @@ ADD = mybir.AluOpType.add
 P = 128
 PACK = 4
 PASSES = K // (P * PACK)
-QUADS = 4
 BANK = 512
 BLOCK = BANK // PACK
 
@@ -346,6 +345,6 @@ def tile_picked_zres_gelu_po_kernel(
         for n0 in (384, 640, 896):
             quantize_result(n0)
 
-        for q in range(QUADS):
-            queue = nc.sync if q % 2 == 0 else nc.scalar
-            queue.dma_start(out_2[0, 4 * q : 4 * q + 4, :].bitcast(I32), out_plane[32 * q : 32 * q + 4, :].bitcast(I32))
+        for r in range(4):
+            queue = nc.sync if r % 2 == 0 else nc.scalar
+            queue.dma_start(out_2[0, r::4, :].bitcast(I32), out_plane[r:P:32, :].bitcast(I32))

@@ -340,9 +340,11 @@ def tile_picked_zres_gelu_po_kernel(
         for b in range(6, 8):
             keep_h(b)
             branch(b * BLOCK, 0, PACK)
-        for b in range(5, 8):
+        for b in range(5, 7):
             round_by(nc.scalar.copy, b * BLOCK, BLOCK)
-        for n0 in (384, 640, 896):
+        quantize_result(384)
+        round_by(nc.vector.tensor_copy, 7 * BLOCK, BLOCK)
+        for n0 in (640, 896):
             quantize_result(n0)
 
         for r in range(4):

@@ -283,10 +283,15 @@ def tile_picked_zres_gelu_po_kernel(
             rounded = result_bf[first][:, (n0 - first) * PACK : (n0 - first + w) * PACK]
             return rounded, quarters_of(result[piece])[:, :, n0 - piece : n0 - piece + w]
 
-        def round_on_gpsimd(n0, w):
+        def round_on_gpsimd(n0, w, run=1):
             rounded, exact = rounding_views(n0, w)
             nc.gpsimd.tensor_scalar(
-                rounded.rearrange("p (n t) -> p n t", t=PACK), exact.rearrange("p t n -> p n t"), 1.0, 0.0, MULT, ADD
+                rounded.rearrange("p (n i t) -> p n t i", i=run, t=PACK),
+                exact.rearrange("p t (n i) -> p n t i", i=run),
+                1.0,
+                0.0,
+                MULT,
+                ADD,
             )
 
         def round_by(copy, n0, w):
@@ -325,7 +330,7 @@ def tile_picked_zres_gelu_po_kernel(
         keep_h(3)
         quantize_result(0)
         quantize_g(384)
-        round_on_gpsimd(128, 2 * BLOCK)
+        round_on_gpsimd(128, 2 * BLOCK, 2)
         keep_h(4)
         wide_branch(384)
 
@@ -335,7 +340,7 @@ def tile_picked_zres_gelu_po_kernel(
         quantize_g(640)
         quantize_g(896)
         quantize_result(128)
-        round_on_gpsimd(384, 2 * BLOCK)
+        round_on_gpsimd(384, 2 * BLOCK, 2)
         branch(640, 0, PACK)
         for b in range(6, 8):
             keep_h(b)

from contextlib import ExitStack

import concourse.mybir as mybir
from concourse.masks import make_identity

K, T, S, H = 1024, 2048, 1024, 512
FLOPS = 2 * K * H * S + 2 * H * H * S

F32 = mybir.dt.float32
BF16 = mybir.dt.bfloat16
I32 = mybir.dt.int32
U32 = mybir.dt.uint32
U16 = mybir.dt.uint16
U8 = mybir.dt.uint8
FP8X4 = mybir.dt.float8_e4m3fn_x4
FP4X4 = mybir.dt.float4_e2m1fn_x4
GELU = mybir.ActivationFunctionType.Gelu_apprx_tanh
MULT = mybir.AluOpType.mult
ADD = mybir.AluOpType.add

P = 128
PACK = 4
PASSES = K // (P * PACK)
BANK = 512
BLOCK = BANK // PACK

FIRST_PIECE = 3 * T // 8
SCALAR_SHARES = (100, 76)
OPEN_BLOCKS = 3
GATHERS = (128, 128, 256, 512)
H_BANKS = 4
Y_BANKS = 3
G_SPANS = ((0, 128), (128, 256), (384, 256), (640, 256), (896, 128))
OUT_SPANS = G_SPANS
PIECES = ((0, 128), (128, 256), (384, 256), (640, 128), (768, 128), (896, 128))
RESULTS = ((0, 384), (384, 256), (640, 128), (768, 256))
H_ON_VECTOR = (0, 4)
STORED = {128: 2, 384: 2, 640: 4, 896: 2}
CODE_STORES = {128: 0, 640: 384, 896: 896}

KIB = 1024
X_ROWS_AT = 0
X_TABLE1_AT = 4 * KIB
HELD = X_TABLE1_AT + 4 * T
PICKED_ROWS_AT = HELD - 128
W2_RAW_AT = HELD + 64
W1_BF_AT = (HELD + 6 * KIB, HELD + 2 * KIB)
W2_PLANE_AT = W1_BF_AT[0]
RING = HELD + 12 * KIB
G_BF_AT = {0: RING, 128: RING + KIB, 384: RING + 3 * KIB, 640: RING + 5 * KIB, 896: RING + 9 * KIB}
RESULT_BF_AT = {
    0: RING + 2 * KIB,
    128: RING + 5 * KIB // 2,
    384: RING + 15 * KIB // 2,
    640: RING + 14 * KIB,
    896: RING + 16 * KIB,
}
HELD_PIECE = 640
HELD_PIECE_AT = RING + 19 * KIB // 2


def tile_picked_zres_gelu_po_kernel(
    tc, x_words, x_scales, w1, w2_words, w2_scales, turn, offs, out_0, out_1, out_2
):
    nc = tc.nc
    with ExitStack() as ctx:
        keep = ctx.enter_context(tc.tile_pool(name="keep", bufs=1))
        shared = ctx.enter_context(tc.tile_pool(name="shared", bufs=1))
        psum = ctx.enter_context(tc.psum_pool(name="psum", bufs=4))

        offsets = keep.tile([P, S // 16], U16, name="offsets")
        x_rows = shared.tile([P, T], U8, name="x_rows", align_bytes=64, offset=X_ROWS_AT)
        w2_rows = keep.tile([P, H], U8, name="w2_rows", align_bytes=64)
        warm = keep.tile([P, 8], F32, name="warm")
        warm_out = keep.tile([P, 8], F32, name="warm_out")
        nc.vector.memset(x_rows[:].bitcast(I32), 0)
        nc.vector.memset(w2_rows[:].bitcast(I32), 0)
        nc.vector.memset(warm[:], 0.0)
        nc.scalar.activation(warm_out[:], warm[:], GELU)
        identity = keep.tile([P, P], F32, name="identity")
        turn_row = keep.tile([P, H], F32, name="turn_row")
        nc.vector.memset(turn_row[:], 0.0)
        nc.vector.memset(identity[:], 0.0)
        make_identity(nc, identity[:], nomemset=True)

        picked_rows = shared.tile([P, S], U8, name="picked_rows", align_bytes=64, offset=PICKED_ROWS_AT)
        w1_raw = [keep.tile([P, PACK, H], F32, name="w1_raw%d" % a) for a in range(PASSES)]
        x_table = [
            keep.tile([P, T], U32, name="x_table0", align_bytes=64),
            shared.tile([P, T], U32, name="x_table1", align_bytes=64, offset=X_TABLE1_AT),
        ]
        w2_raw = shared.tile([P, 2 * H], U8, name="w2_raw", align_bytes=64, offset=W2_RAW_AT)
        x_planes = [keep.tile([P, S], U8, name="x_plane%d" % a, align_bytes=64) for a in range(PASSES)]

        def load_w1(a):
            rows = w1[a * P * PACK : (a + 1) * P * PACK, :].rearrange("(p j) c -> p j c", j=PACK)
            nc.sync.dma_start(w1_raw[a][:], rows)

        def load_x(a, n0, n1):
            words = x_words[a].rearrange("p n t -> p (n t)").bitcast(I32)
            nc.sync.dma_start(x_table[a][:, n0:n1].bitcast(I32), words[:, n0:n1])

        def place_rows(plane, first):
            for r in range(1, 4):
                nc.sync.dma_start(
                    plane[first + r : P : 32, :].bitcast(I32), plane[first + 8 * r : P : 32, :].bitcast(I32)
                )

        load_x(0, 0, FIRST_PIECE)
        nc.sync.dma_start(offsets[:], offs)
        nc.sync.dma_start(x_rows[0:P:4, :].bitcast(I32), x_scales.bitcast(I32).rearrange("a q n -> q a n"))
        nc.scalar.dma_start(w2_rows[0:P:8, :].bitcast(I32), w2_scales[0].bitcast(I32))
        load_x(0, FIRST_PIECE, T)
        nc.scalar.dma_start(turn_row[0:1, :], turn.rearrange("m o -> o m"))
        load_w1(0)
        load_w1(1)
        nc.vector.tensor_copy(picked_rows[:], x_rows[:].indirect(offsets[:]))
        for a in range(PASSES):
            nc.vector.tensor_copy(x_planes[a][:].bitcast(I32), picked_rows[:].bitcast(I32))
        place_rows(x_planes[0], 0)
        load_x(1, 0, T)
        nc.sync.dma_start(w2_raw[:].bitcast(I32), w2_words[0].bitcast(I32))
        place_rows(x_planes[1], 4)
        factor = psum.tile([P, PACK, P], F32, name="factor", bufs=1)
        for t in range(PACK):
            nc.tensor.transpose(factor[:, t, :], turn_row[:, t:H:PACK], identity[:])

        w1_bf = [
            shared.tile([P, H * PACK], BF16, name="w1_bf%d" % a, align_bytes=64, offset=W1_BF_AT[a])
            for a in range(PASSES)
        ]
        w1_codes = [keep.tile([P, H], U32, name="w1_codes%d" % a, align_bytes=64) for a in range(PASSES)]
        w1_plane = [keep.tile([P, H], U8, name="w1_plane%d" % a, align_bytes=64) for a in range(PASSES)]
        w2_plane = shared.tile([P, H], U8, name="w2_plane", align_bytes=64, offset=W2_PLANE_AT)
        w2_codes = keep.tile([P, 2 * H], U8, name="w2_codes", align_bytes=64)

        def quantize_w1(a):
            dst = w1_bf[a][:].rearrange("p (t m j) -> p m j t", t=PACK, j=PACK)
            src = w1_raw[a][:].rearrange("p j (m t) -> p m j t", t=PACK)
            share = SCALAR_SHARES[a]
            nc.scalar.copy(dst[:, :share], src[:, :share])
            nc.vector.tensor_copy(dst[:, share:], src[:, share:])
            nc.vector.quantize_mx(w1_codes[a][:].bitcast(FP8X4), w1_plane[a][:], w1_bf[a][:])

        x_picked = {}

        def gather_x(a, n0, picked):
            n1 = n0 + picked.shape[1]
            nc.vector.tensor_copy(picked, x_table[a][:].indirect(offsets[:, n0 // 16 : n1 // 16]))
            for n in range(n0, n1, BLOCK):
                x_picked[a, n] = picked[:, n - n0 : n - n0 + BLOCK]

        first_picked = shared.tile([P, S], U32, name="first_picked", align_bytes=64, offset=X_ROWS_AT)
        gather_x(0, 0, first_picked[:])
        quantize_w1(0)
        nc.vector.tensor_copy(
            w2_plane[:].rearrange("p (t m) -> p t m", t=PACK),
            w2_rows[:].rearrange("p (m t) -> p t m", t=PACK),
        )
        place_rows(w2_plane, 0)

        h_banks = {}

        def product_pass(n0, a, opens):
            for t in range(PACK):
                nc.tensor.matmul_mx(
                    h_banks[n0][:, t, :],
                    lhsT=w1_codes[a][:, t * P : (t + 1) * P].bitcast(FP8X4),
                    lhsT_scale=w1_plane[a][:, t * P : (t + 1) * P],
                    rhs=x_picked[a, n0].bitcast(FP8X4),
                    rhs_scale=x_planes[a][4 * a : P, n0 : n0 + BLOCK],
                    start=(opens and t == 0),
                    stop=(not opens and t == PACK - 1),
                )

        def open_block(n0, a):
            h_banks[n0] = psum.tile([P, PACK, BLOCK], F32, name="h_bank", bufs=H_BANKS)
            product_pass(n0, a, True)

        for n0 in range(0, OPEN_BLOCKS * BLOCK, BLOCK):
            open_block(n0, 0)

        quantize_w1(1)
        last_picked = keep.tile([P, S], U32, name="last_picked", align_bytes=64)
        for i, width in enumerate(GATHERS):
            n0 = sum(GATHERS[:i])
            gather_x(1, n0, last_picked[:, n0 : n0 + width])

        nc.scalar.copy(
            w2_codes[:].bitcast(U16).rearrange("p (t m) -> p m t", t=PACK),
            w2_raw[:].bitcast(U16).rearrange("p (m t) -> p m t", t=PACK),
        )

        out_codes = keep.tile([P, S], U32, name="out_codes", align_bytes=64)
        out_plane = keep.tile([P, S], U8, name="out_plane", align_bytes=64)
        out_rows = out_0.rearrange("(p t) n -> p t n", t=PACK)
        out_words = out_1[0].rearrange("p n t -> p (n t)").bitcast(I32)

        def kept_tiles(name, dtype, per_token, spans):
            return {
                n0: keep.tile([P, w * per_token], dtype, name="%s%d" % (name, n0), align_bytes=64) for n0, w in spans
            }

        def staged_tiles(name, at, spans):
            return {
                n0: shared.tile([P, w * PACK], BF16, name="%s%d" % (name, n0), align_bytes=64, offset=at[n0])
                for n0, w in spans
            }

        def span_of(spans, n):
            return max(span for span in spans if span[0] <= n)

        def quarters_of(tile):
            return tile[:].rearrange("p (t n) -> p t n", t=PACK)

        g_bf = staged_tiles("g_bf", G_BF_AT, G_SPANS)
        g_codes = kept_tiles("g_codes", U32, 1, G_SPANS)
        g_plane = kept_tiles("g_plane", U8, 1, G_SPANS)
        h_kept = kept_tiles("h_kept", F32, PACK, PIECES)
        result = kept_tiles("result", F32, PACK, [span for span in RESULTS if span[0] != HELD_PIECE])
        result[HELD_PIECE] = shared.tile([P, BANK], F32, name="result_held", align_bytes=64, offset=HELD_PIECE_AT)
        result_bf = staged_tiles("result_bf", RESULT_BF_AT, OUT_SPANS)

        def project(b):
            n0 = b * BLOCK
            if n0 in h_banks:
                product_pass(n0, 1, False)
            else:
                open_block(n0, 1)
                product_pass(n0, 0, False)
            first = span_of(G_SPANS, n0)[0]
            local = n0 - first
            nc.scalar.activation(
                g_bf[first][:, local * PACK : (local + BLOCK) * PACK].rearrange("p (n t) -> p n t", t=PACK),
                h_banks[n0][:].rearrange("p t n -> p n t"),
                GELU,
            )

        def keep_h(b):
            n0 = b * BLOCK
            first = span_of(PIECES, n0)[0]
            dst = quarters_of(h_kept[first])[:, :, n0 - first : n0 - first + BLOCK]
            if b in H_ON_VECTOR:
                nc.vector.tensor_copy(dst, h_banks[n0][:])
            else:
                nc.scalar.copy(dst, h_banks[n0][:])

        def quantize_g(n0):
            nc.vector.quantize_mx(g_codes[n0][:].bitcast(FP8X4), g_plane[n0][:], g_bf[n0][:])

        def branch(n0, t0, t1):
            w = span_of(PIECES, n0)[1]
            first = span_of(G_SPANS, n0)[0]
            cols = slice(n0 - first, n0 - first + w)
            r0, rw = span_of(RESULTS, n0)
            bank = psum.tile([P, BANK], F32, name="y_bank", bufs=Y_BANKS)
            for t in range(t0, t1):
                nc.tensor.matmul_mx(
                    bank[:, (t - t0) * w : (t - t0 + 1) * w],
                    lhsT=w2_codes[:, t * 2 * P : (t + 1) * 2 * P].bitcast(FP4X4),
                    lhsT_scale=w2_plane[:, t * P : (t + 1) * P],
                    rhs=g_codes[first][:, cols].bitcast(FP8X4),
                    rhs_scale=g_plane[first][:, cols],
                    start=True,
                    stop=True,
                )
            for t in range(t0, t1):
                nc.vector.scalar_tensor_tensor(
                    quarters_of(result[r0])[:, t, n0 - r0 : n0 - r0 + w],
                    bank[:, (t - t0) * w : (t - t0 + 1) * w],
                    factor[:, t, 0:1],
                    quarters_of(h_kept[n0])[:, t, :],
                    MULT,
                    ADD,
                )
                if n0 in STORED and (t + 1) % STORED[n0] == 0:
                    quarters = slice(t + 1 - STORED[n0], t + 1)
                    nc.sync.dma_start(out_rows[:, quarters, r0 : r0 + rw], quarters_of(result[r0])[:, quarters, :])

        def rounding_views(n0, w):
            piece = span_of(RESULTS, n0)[0]
            first = span_of(OUT_SPANS, n0)[0]
            rounded = result_bf[first][:, (n0 - first) * PACK : (n0 - first + w) * PACK]
            return rounded, quarters_of(result[piece])[:, :, n0 - piece : n0 - piece + w]

        def round_on_gpsimd(n0, w, run=1):
            rounded, exact = rounding_views(n0, w)
            nc.gpsimd.tensor_scalar(
                rounded.rearrange("p (n i t) -> p n t i", i=run, t=PACK),
                exact.rearrange("p t (n i) -> p n t i", i=run),
                1.0,
                0.0,
                MULT,
                ADD,
            )

        def round_by(copy, n0, w):
            rounded, exact = rounding_views(n0, w)
            copy(
                rounded.rearrange("p (n i t) -> p n t i", i=4, t=PACK), exact.rearrange("p t (n i) -> p n t i", i=4)
            )

        def quantize_result(n0):
            cols = slice(n0, n0 + span_of(OUT_SPANS, n0)[1])
            nc.vector.quantize_mx(out_codes[:, cols].bitcast(FP8X4), out_plane[:, cols], result_bf[n0][:])
            if n0 in CODE_STORES:
                cols = slice(CODE_STORES[n0], cols.stop)
                nc.sync.dma_start(out_words[:, cols], out_codes[:, cols].bitcast(I32))

        half = PACK // 2

        def wide_branch(n0):
            branch(n0, 0, half)
            branch(n0, half, PACK)

        project(0)
        project(1)
        quantize_g(0)
        keep_h(0)
        project(2)
        quantize_g(128)
        branch(0, 0, PACK)
        keep_h(1)
        round_on_gpsimd(0, BLOCK)
        keep_h(2)
        wide_branch(128)

        project(3)
        project(4)
        keep_h(3)
        quantize_result(0)
        quantize_g(384)
        round_on_gpsimd(128, 2 * BLOCK, 2)
        keep_h(4)
        wide_branch(384)

        for b in range(5, 8):
            project(b)
        keep_h(5)
        quantize_g(640)
        quantize_g(896)
        quantize_result(128)
        round_on_gpsimd(384, 2 * BLOCK, 2)
        branch(640, 0, PACK)
        for b in range(6, 8):
            keep_h(b)
            branch(b * BLOCK, 0, PACK)
        for b in range(5, 7):
            round_by(nc.scalar.copy, b * BLOCK, BLOCK)
        quantize_result(384)
        round_by(nc.vector.tensor_copy, 7 * BLOCK, BLOCK)
        for n0 in (640, 896):
            quantize_result(n0)

        for r in range(4):
            queue = nc.sync if r % 2 == 0 else nc.scalar
            queue.dma_start(out_2[0, r::4, :].bitcast(I32), out_plane[r:P:32, :].bitcast(I32))
